import numpy as np, ml_dtypes
CORES = [3,11,19,27,35,43,51,59]
N = 8
BF = ml_dtypes.bfloat16
def gentries(a):
    return np.ascontiguousarray(a.reshape(8, 16, -1).transpose(0, 2, 1)).reshape(8, -1)
def gtable(e):
    e = np.asarray(e); return np.ascontiguousarray(e.reshape(8, -1, 16).transpose(0, 2, 1)).reshape(128, -1).astype(np.int32)
def f(rng, *shape):
    return (rng.standard_normal(shape, dtype=np.float32) * np.exp2(rng.integers(-2, 3, shape[:-1] + (1,)))).astype(BF)
def wide(rng, *shape):
    v = f(rng, *shape).astype(np.float32); k = shape[:-2] + (1, shape[-1])
    return (v * np.exp2(rng.integers(-6, 7, k)) * (rng.random(k) > 0.0625)).astype(BF)
W, R, TK, A = 2048, 1536, 3, 128
X = np.arange(16)[:, None]
def cols(rng, lo, hi, lead, m=16):
    sh = rng.integers(lo, hi, lead + (1, W)); z = np.zeros(lead + (1, W), np.int64)
    c = np.sort((rng.integers(0, 257, lead + (m - 1, W)) >> sh) << sh, axis=-2)
    v = np.diff(np.concatenate([z, c, z + 256], axis=-2), axis=-2)
    return np.take_along_axis(v, np.argsort(rng.random(v.shape), axis=-2), -2)
def parts(rng, lo=0, hi=8):
    P = cols(rng, lo, hi, (8,)); a = cols(rng, lo, hi, (N, 8)); m = (P + a) >> 1
    m = m + (256 - np.add.reduce(m, axis=-2, keepdims=True)) * (X == rng.integers(0, 16, (N, 8, 1, W)))
    return {"P": P, "Q": np.where(rng.random((N, 8, 1, W)) < 0.5, m, a), "E": rng.integers(0, A, (8, 16, W)), "V": np.clip(f(rng, 128, W).astype(np.float32), -2, 2),
            "n": rng.integers(0, W, (N, 8, R)), "s": np.argsort(rng.random((N, 8, TK, W)), axis=-1)[..., :R], "d": rng.integers(0, 256, (N, 8, TK, 2, R)), "a": rng.integers(0, 128, (N, 8, TK, 3, R))}
def pack(v):
    def small(a): return np.ascontiguousarray(a).astype(np.float32).astype(BF)
    def alike(a): return small(np.stack([np.reshape(a, (128, W))] * N))
    return {"pt": alike(v["P"]), "qd": small(v["Q"].reshape(N, 128, W)), "nx": alike(v["E"]), "vf": alike(v["V"]), "n0": np.stack([gtable(a) for a in v["n"]]),
            "spot": np.stack([gtable(a.reshape(8, -1)) for a in v["s"]]), "ud": small(v["d"].reshape(N, 8, 2 * TK * R)), "ua": small(v["a"].reshape(N, 8, 3 * TK * R))}
def setup_inputs(rng):
    return pack(parts(rng))
def setup_inputs_spread(rng):
    v = parts(rng, 0, 9); v["V"] = np.clip(wide(rng, 128, W).astype(np.float32) * 0.5, -2, 2)
    r = rng.random((N, 8, R)); v["n"] = (W * r * r * r).astype(np.int64); r = rng.random((8, 16, W)); v["E"] = (A * r * r).astype(np.int64)
    r = rng.random(v["d"].shape); v["d"] = (256 * np.where(rng.random((N, 8, TK, 2, 1)) < 0.5, r * r, 1 - r * r * r)).astype(np.int64) & 255
    r = rng.random(v["a"].shape); v["a"] = (128 * np.where(rng.random((N, 8, TK, 3, 1)) < 0.5, r * r, 1 - r * r * r)).astype(np.int64) & 127
    return pack(v)
def two(rng, lead):
    a = rng.integers(0, 16, lead + (1, W)); b = (a + rng.integers(1, 16, lead + (1, W))) & 15; k = rng.choice(np.array([256, 256, 256, 255, 128, 1]), lead + (1, W))
    return k * (X == a) + (256 - k) * (X == b)
def setup_inputs_ends(rng):
    v = parts(rng); v["P"] = two(rng, (8,)); v["Q"] = two(rng, (N, 8)); x = np.arange(16)
    v["P"][7, :, W - 1] = 256 * (x == 15); v["Q"][:, 7, :, W - 1] = 256 * (x == 0); v["P"][2, :, 0] = 256 * (x == 14); v["Q"][:, 2, :, 0] = 256 * (x == 1)
    v["E"] = (A - 1) * rng.integers(0, 2, (8, 16, W)); v["V"] = 4.0 * rng.integers(0, 2, (128, W)) - 2.0
    v["n"] = (W - 1) * rng.integers(0, 2, (N, 8, R)); v["n"][:, :, R - 1] = W - 1; v["n"][:, :, 0] = 0
    ends = np.concatenate([np.arange(R // 2), np.arange(W - R // 2, W)]); v["s"] = ends[np.argsort(rng.random((N, 8, TK, R)), axis=-1)]
    v["d"] = 255 * rng.integers(0, 2, v["d"].shape); v["a"] = 127 * rng.integers(0, 2, v["a"].shape)
    return pack(v)
def odd(v, par):
    return np.where((X & 1) == par, np.repeat(v, 2, axis=-2), 0)
def setup_inputs_corners(rng):
    v = parts(rng); par = rng.integers(0, 2, (8, 1, W)); D = odd(cols(rng, 0, 8, (N, 8), 8), 1 - par)
    y = np.arange(8)[:, None]; i = rng.integers(0, 8, (8, 1, W)); j = (i + rng.integers(1, 8, (8, 1, W))) & 7; b = rng.integers(1, 65, (8, 1, W))
    P = odd(np.where(rng.random((8, 1, W)) < 0.4, (256 - b) * (y == i) + b * (y == j), cols(rng, 0, 8, (8,), 8)), par)
    top = (X == np.argmax(P, axis=-2)[..., None, :]) * 1; big = (X == np.argmax(D, axis=-2)[..., None, :]) * 1
    rest = P * (1 - top); nxt = (X == np.argmax(rest, axis=-2)[..., None, :]) * 1
    D = D + rng.integers(0, 2, (N, 8, 1, W)) * (top - big); edge = (X == np.where(par == 1, 0, 15)) * 1
    k = rng.integers(1, 4, (N, 8, 1, W)); both = ((k >= 2) & (np.max(rest, axis=-2, keepdims=True) >= 1)) * 1
    near = P + k * (edge - top) + both * (top - nxt)
    kind = np.array([0, 1, 1, 2, 3, 2, 0, 3])[(np.arange(N)[:, None] + np.arange(8)) & 7][:, :, None, None]
    v["P"] = P; v["Q"] = np.where(kind == 0, P, np.where(kind == 1, D, np.where(kind == 2, near, v["Q"])))
    v["d"] = np.where(rng.random(v["d"].shape) < 0.7, rng.choice(np.array([0, 1, 2, 3, 252, 253, 254, 255]), v["d"].shape), v["d"])
    v["a"] = np.where(rng.random(v["a"].shape) < 0.7, rng.choice(np.array([0, 1, 126, 127]), v["a"].shape), v["a"])
    v["n"] = np.where(rng.random(v["n"].shape) < 0.2, rng.choice(np.array([0, W - 1]), v["n"].shape), v["n"])
    v["E"] = np.where(rng.random(v["E"].shape) < 0.2, rng.choice(np.array([0, A - 1]), v["E"].shape), v["E"])
    return pack(v)
def setup_inputs_ties(rng):
    v = parts(rng); P = cols(rng, 4, 8, (8,)); Q = np.where(rng.random((N, 8, 1, W)) < 0.33, P, cols(rng, 4, 8, (N, 8)))
    o = np.argsort(rng.random((8, 16, W)), axis=-2); k = rng.choice(np.array([41, 47, 55, 61]), (8, 1, W)); i = rng.integers(0, 4, (N, 8, 1, W)); own = rng.random((8, 1, W)) < 0.4
    one = 256 * (o == 4); half = 128 * ((o == i) | (o == ((i + 1) & 3)))
    v["P"] = np.where(own, np.where(o < 4, k, (256 - 4 * k) * (o == 4)), P)
    v["Q"] = np.where(own, np.where(rng.random((N, 8, 1, W)) < 0.5, one, half), Q)
    v["d"] = np.clip(16 * rng.integers(0, 17, v["d"].shape) - rng.integers(0, 2, v["d"].shape), 0, 255)
    v["a"] = rng.choice(np.array([0, 16, 31, 32, 33, 48, 63, 64, 65, 80, 96, 112, 127]), v["a"].shape)
    v["a"][:, :, :, 1] = np.where(rng.random((N, 8, TK, R)) < 0.3, 64, v["a"][:, :, :, 1])
    return pack(v)
def setup_inputs_alike(rng):
    v = parts(rng); c = rng.integers(0, W - 1, (N, 8, 1)); v["n"] = c + np.zeros((N, 8, R), np.int64); v["n"][:, 1::2, R - 1] += 1
    b = rng.integers(0, A - 3, (8, 1, 1)); v["E"] = b + 3 * rng.integers(0, 2, (8, 16, W))
    k = rng.integers(0, W, 64)[rng.integers(0, 64, W)]; v["P"] = v["P"][:, :, k]
    return pack(v)
def check_ranges(d):
    bad = []
    for k, lo, hi in (("pt", 0, 256), ("qd", 0, 256), ("nx", 0, A - 1), ("vf", -2, 2), ("n0", 0, W - 1), ("spot", 0, W - 1), ("ud", 0, 255), ("ua", 0, 127)):
        a = np.asarray(d[k]).astype(np.float64)
        if not (np.min(a) >= lo and np.max(a) <= hi): bad.append("range of " + k)
        if k != "vf" and not np.all(a == np.floor(a)): bad.append("whole numbers of " + k)
        if k in ("pt", "nx", "vf") and not np.all(a == a[:1]): bad.append(k + " alike on all ranks")
        if k in ("pt", "qd") and not np.all(np.add.reduce(a.reshape(N, 8, 16, W), axis=2) == 256): bad.append("sums of " + k)
    s = np.sort(np.stack([gentries(np.asarray(a)) for a in d["spot"]]).reshape(N, 8, TK, R), axis=-1)
    if np.any(s[..., 1:] == s[..., :-1]): bad.append("repeated places in spot")
    return bad
def pick(tab, n):
    return np.take_along_axis(tab, n[:, :, None, :], 3)
def at(v, x):
    return np.take_along_axis(v, x[:, :, None, :], 2)[:, :, 0]
def first(m):
    return np.argmax(m, axis=2)
def teach(Q, rej, pl, p):
    for r in range(N):
        for g in range(8):
            k = rej[r, g]; Q[r, g][:, pl[r, g, k]] = p[r, g][:, k]
def reference(pt, qd, nx, vf, n0, spot, ud, ua):
    def ints(a): return a.astype(np.float32).astype(np.int64)
    P = ints(pt).reshape(N, 8, 16, W); Q = ints(qd).reshape(N, 8, 16, W); E = ints(nx).reshape(N, 8, 16, W); v = vf.astype(np.float64).reshape(N, 8, 16, W)
    n = np.stack([gentries(a) for a in n0]).astype(np.int64); pl = np.stack([gentries(a) for a in spot]).astype(np.int64).reshape(N, 8, TK, R)
    u = ints(ud).reshape(N, 8, TK, 2, R); w = ints(ua).reshape(N, 8, TK, 3, R); h = np.zeros((N, 8, 16, R)); seen = []
    for t in range(TK):
        p = pick(P, n); q = pick(Q, n)
        x = first(np.add.accumulate(q, axis=2) > u[:, :, t, 0][:, :, None])
        rej = w[:, :, t, 0] * at(q, x) >= 128 * at(p, x)
        p1 = np.maximum(p - q, 0)
        teach(Q, rej, pl[:, :, t], p)
        n, x, rej, p1, h = [np.roll(a, 1, axis=0) for a in (n, x, rej, p1, h)]
        s = np.add.reduce(p1, axis=2); p = pick(P, n); q = pick(Q, n)
        y = first(np.add.accumulate(q, axis=2) > u[:, :, t, 1][:, :, None])
        again = rej & (w[:, :, t, 1] * at(q, y) * s >= 32768 * at(p1, y))
        c = np.add.accumulate(np.maximum(256 * p1 - s[:, :, None] * q, 0), axis=2)
        z = first(128 * c > w[:, :, t, 2][:, :, None] * c[:, :, 15:])
        x = np.where(again, z, np.where(rej, y, x))
        if t < TK - 1: teach(Q, again, pl[:, :, t], p)
        row = np.concatenate([x[:, :1], (x[:, 1:] + x[:, :-1]) & 15], axis=1)
        n = 16 * at(pick(E, n), row) + x
        h = np.tanh(h + pick(v, n)); seen.append(n)
    yn = np.stack(seen, axis=2).reshape(N, 8, TK * R)
    return {"yh": h.reshape(N, 128, R).astype(np.float32), "yn": np.stack([gtable(a) for a in yn]).astype(np.float32)}

def check_inputs(d):
    bad = list(check_ranges(d))
    if not bad:
        for name, y in reference(**d).items():
            for q in range(N):
                v = np.abs(np.asarray(y[q], np.float64)); s = np.sqrt(np.mean(v * v))
                if v.max() > 3 * s or s < 2.0 ** -3: bad.append('%s of rank %d is uneven or too small' % (name, q))
    return bad

@@ -1,0 +1,499 @@
+from concourse.bass import DstId, RemoteDMATransfer
+from concourse.mybir import AluOpType, ActivationFunctionType
+
+ALU = AluOpType
+ACT = ActivationFunctionType
+R, W, TK, C = 1536, 2048, 3, 96
+DIGITS = "0123456789abcdefghijklmnopqrstuv"
+
+CFG = {
+    "chunks": [512, 512, 512], "chb": [512, 512, 512],
+    "ga":[[0],[1,2]],"gb":[[0],[1],[2]],"gr":[[0],[1,2]],"gq":["SVV","SVS","SVV"],"gp":["VSV","VSS","SSV"],"gq2":["SVS","SVS","SVS"],"ge":["SSS","SSS","SSS"],"selq":["VSS","VVS","VVS"],"selp":["SVS","VVV","VSS"],"selq2":["VVV","VVS","VVV"],"selr":["VSV","VSS","VVV"],"sele":["SSV","SSV","VVV"],"h2":"dma","acc":["VVV","VVV","VVV"],"loads":"ndaqpseADv","zpe":0,"piece":1024,
+    "order":"0b000c0j0n0o010a020i030f0g0k0p0s0h21040506070809131b0d0l0r160t0u150v0q1m17183e191k1n1v1c1o0e1d0m10221p231a1r1e1l1f1g201i1h241q1s2d2514261j2e2f2g1t272h2b2q283j2i1u292j2k2c2n2l2m2r40452o472p4h3a2a343l11333k463b3m353s3c363t3d374812303u3g493f3v4a383n3h4c2t393o3i4d4b3q2s4m3r3p41325m4e2u4s564f4n4g5n4o42312v5o4q4j4p575p584t4i435a594r5q644k444u4l5c4v5b505s5d655e51695f5r5g5t665u525h5v6a535i6b5j54606c6e5k6o6m6n6f616d6g6p6h6q626k6j68706r676i72716s737e6t746u7f7g63777h6v7i75787r79767a7j6l7d7t7c9b7k7o7l7m7n7s94887p86bd7q7b7v558ibf5l8o9a9i908p87919c8q9j9d89928a8e8f938b8c8r968d84958s8u8g979k8h808v8t98838jbe9r818n7u82ab9s8k859l9t9v9g9uaca0ad9eb98l9m8m9o9n99afagaea19f9pa2a3ahba9h9qara4a5b1asaiatauajavbsakb0c7alb2bba6b3a7ama8anb4aoa9b5bgbiapb6bhbqbjaab7bobkbcc5brblbtbnc8bpc3bmbucgc6cic9bvcjc4c1ckc0cac2clcmcccvcbcecdcfcnd3chehcoaqd2cscpcqcrd0ercte0b8cud1dfdldpd4dedvenegdme1dgdne2eie6eodoe3epdbdrejdqeqe7ekdhetesemdid5dsdjddefdkeuele5f0d8evdce8dteafoe4d9e9f4dudaebfsd6f1ecfpf2fqf3d7frf5ftf6fcf7f8fuedfvfdg0f9eefefgfaffg5g1fhg6fig2fjg3g7fkgbflgcfmg8fbgdfng4g9ga",
+    "banks":"0123456723107256103725615234165236405126374501623547625762357624370152012652104365724061357204375247561427561402531072546572013645721",
+}
+
+BF, F32, I32, U16 = "bfloat16", "float32", "int32", "uint16"
+SB = {
+    "qw": (BF, 2 * W), "ptab": (BF, W), "etab": (BF, W), "vtab": (BF, W), "uds": (BF, 6 * R), "uas": (BF, 9 * R),
+    "n0s": (I32, C), "sps": (I32, 3 * C), "s2k": (F32, 3 * C), "cd": (F32, 6 * C),
+    "n16": (U16, 4 * C), "nin": (U16, 4 * C), "off1": (U16, C), "off2": (U16, C), "k16": (U16, C),
+    "q1": (BF, R), "q2": (BF, R), "ecol": (BF, R), "hot": (BF, R), "sele": (BF, R), "v2": (BF, R),
+    "sel1": (BF, 2 * R), "sel2": (BF, 2 * R), "s23": (BF, 2 * R), "pp": (BF, 3 * R), "s1r": (BF, 6 * R),
+    "rin": (BF, 3 * R), "pin": (BF, 2 * R), "msg": (BF, 9 * C), "mi": (BF, 9 * C),
+    "ww": (F32, R), "ew": (F32, R), "sq": (F32, R), "hh": (F32, R), "hs": (F32, R), "ho": (F32, R),
+    "t1": (F32, C), "z1": (F32, C), "t2": (F32, C), "z2": (F32, C), "ds": (F32, C), "ab": (F32, C), "xx": (F32, C),
+    "zs": (F32, C), "rej": (F32, C), "aa": (BF, C), "beta": (BF, 2 * C), "prod": (BF, 2 * C), "nf": (F32, 3 * C),
+    "one": (BF, 160), "half": (BF, 160), "neg": (BF, 128), "blk0": (BF, 144), "blk": (BF, 144), "tri": (BF, 128),
+    "zz": (BF, 144), "z8": (BF, 144), "nsel": (BF, 128), "wh": (BF, 160), "nwh": (BF, 128), "dm0": (BF, 128),
+    "dm1": (BF, 128), "dm2": (BF, 128), "dm": (BF, 128), "sh": (BF, 128), "blkn": (BF, 128), "trif": (F32, 128),
+    "blkf": (F32, 128), "whf": (F32, 128), "id0": (I32, 32), "id1": (I32, 32), "idv": (BF, 32), "ids": (BF, 32),
+    "kc": (F32, 4),
+}
+SIZE = {BF: 2, F32: 4, I32: 4, U16: 2}
+SCRATCH = {k: ("sbuf", [128, v[1]], v[0]) for k, v in SB.items()}
+for _b in range(8):
+    SCRATCH["bank%d" % _b] = ("psum", [128, 512], "float32")
+
+
+def A(name, a, b, step=1, rows=128):
+    return ("ap", name, a, b, step, rows)
+
+
+def X(win, off):
+    return ("ind", win, off)
+
+
+def D(name, a=None, b=None):
+    return ("dram", name, a, b)
+
+
+def parts_of(x):
+    if isinstance(x, tuple) and x[0] == "ap":
+        return [x]
+    if isinstance(x, tuple) and x[0] == "ind":
+        return [x[1], x[2]]
+    return []
+
+
+def count_of(x):
+    return 16 * (x[2][3] - x[2][2]) if x[0] == "ind" else len(range(x[2], x[3], x[4]))
+
+
+def graph(cfg):
+    ops, seen, nt = [], {}, [0]
+
+    def temp():
+        nt[0] += 1
+        return "@%d" % nt[0]
+
+    def add(name, eng, call, args, outs, ins, soft=(), **kw):
+        i = len(ops)
+        deps, acc = set(), []
+        for o in outs:
+            ps = parts_of(o)
+            acc += [(ps[0], True)] + [(p, False) for p in ps[1:]] if ps else []
+        for o in ins:
+            acc += [(p, False) for p in parts_of(o)]
+        for p, wr in acc:
+            bank = p[1][0] == "@"
+            for (a, b, j, w2, rows) in seen.get(p[1], []):
+                if bank:
+                    if wr or w2 or ops[j]["eng"] != eng:
+                        deps.add(j)
+                elif a < p[3] and p[2] < b and (wr or w2) and not (isinstance(rows, tuple) and isinstance(p[5], tuple)):
+                    deps.add(j)
+        for p, wr in acc:
+            seen.setdefault(p[1], []).append((p[2], p[3], i, wr, p[5]))
+        deps.discard(i)
+        op = {"i": i, "name": name, "eng": eng, "call": call, "args": args, "deps": deps, "soft": set(soft),
+              "temps": sorted({p[1] for p, _w in acc if p[1][0] == "@"}), "kind": "c"}
+        op.update(kw)
+        ops.append(op)
+        return i
+
+    def mm(name, out, terms, start=True, stop=True, soft=()):
+        return add(name, "P", "mm", (out, terms, start, stop), [out], [x for t in terms for x in t], soft)
+
+    def tt(name, out, a, b, op):
+        return add(name, "V", "tt", (out, a, b, op), [out], [a, b])
+
+    def ts(name, out, a, s1, s2, op0, op1=None):
+        return add(name, "V", "ts", (out, a, s1, s2, op0, op1), [out], [a, s1, s2])
+
+    def cp(name, out, a):
+        return add(name, "V", "cp", (out, a), [out], [a])
+
+    def act(name, out, a, func, bias=0.0, scale=1.0):
+        return add(name, "S", "act", (out, a, func, bias, scale), [out], [a])
+
+    def gather(name, eng, out, a):
+        return cp(name, out, a) if eng == "V" else act(name, out, a, ACT.Copy)
+
+    def fill(name, out, v):
+        return add(name, "V", "fill", (out, v), [out], [])
+
+    def select(name, out, a, pat, op, base, cm):
+        return add(name, "G", "sel", (out, a, pat, op, base, cm), [out], [a])
+
+    def dma(name, eng, out, a, sem, nbytes, accum=False, soft=()):
+        return add(name, eng, "dma", (out, a, accum), [out], [a] + ([out] if accum else []), soft, kind="dma", sem=sem,
+                   nbytes=nbytes)
+
+    def send(name, out, a, hop):
+        return add(name, "G", "send", (out, a, hop), [out], [a], kind="send", sem=name,
+                   nbytes=128 * count_of(a) * SIZE[SB[a[1]][0]])
+
+    def whole(n, rows=128):
+        return A(n, 0, SB[n][1], 1, rows)
+
+    ch = []
+
+    def cut(sizes):
+        ch[:] = [(sum(sizes[:k]), sum(sizes[:k + 1])) for k in range(len(sizes))]
+
+    def span(grp):
+        return ch[grp[0]][0], ch[grp[-1]][1]
+
+    def pair(groups, which, j):
+        for grp in groups:
+            if j in grp:
+                a, b = span(grp)
+                o = 2 * a + which * (b - a) + ch[j][0] - a
+                return o, o + ch[j][1] - ch[j][0]
+
+    def pieces(groups):
+        out = []
+        for grp in groups:
+            a, b = span(grp)
+            out += [(x, min(b, x + cfg["piece"])) for x in range(a, b, cfg["piece"])]
+        return out
+
+    def to_list(buf, a, b):
+        return [(A("zz", 15 - m, 143 - m), A(buf, a + m, b, 16)) for m in range(16)]
+
+    WH, QW, QR = A("wh", 16, 144), whole("qw"), A("qw", 0, W)
+    TRI, NSEL, DM = whole("tri"), whole("nsel", 8), whole("dm")
+
+    loads = {"n": (whole("n0s"), D("n0"), 128 * C * 4), "q": (QR, D("qd"), 128 * W * 2),
+             "p": (whole("ptab"), D("pt"), 128 * W * 2), "d": (A("uds", 0, 2 * R, 1, 8), D("ud", 0, 2 * R), 8 * 4 * R),
+             "D": (A("uds", 2 * R, 6 * R, 1, 8), D("ud", 2 * R, 6 * R), 8 * 8 * R),
+             "a": (A("uas", 0, 3 * R, 1, 8), D("ua", 0, 3 * R), 8 * 6 * R),
+             "A": (A("uas", 3 * R, 9 * R, 1, 8), D("ua", 3 * R, 9 * R), 8 * 12 * R),
+             "s": (whole("sps"), D("spot"), 128 * C * 12),
+             "e": (whole("etab"), D("nx"), 128 * W * 2), "v": (whole("vtab"), D("vf"), 128 * W * 2)}
+    prev = []
+    for k in cfg["loads"]:
+        prev = [dma("ld_" + k, "Y", loads[k][0], loads[k][1], "ld%d" % ord(k), loads[k][2], soft=prev)]
+    fill("one", whole("one"), 1.0)
+    fill("neg", whole("neg"), -1.0)
+    fill("half", whole("half"), 0.5)
+    fill("kc0", whole("kc"), 16.0)
+    fill("kc1", whole("kc", 16), 8.0)
+    select("blk0", whole("blk0"), A("one", 0, 144), [[-16, 9], [0, 16]], ALU.is_ge, 0, 1)
+    select("blk", whole("blk"), whole("blk0"), [[16, 9], [0, 16]], ALU.is_ge, 15, -1)
+    select("tri", TRI, A("blk", 0, 128), [[1, 128]], ALU.is_ge, 0, -1)
+    select("nsel", NSEL, whole("neg", 8), [[1, 8], [0, 16]], ALU.is_equal, 0, -1)
+    select("wh", whole("wh"), whole("half"), [[1, 160]], ALU.is_equal, -16, -1)
+    select("z8", whole("z8", 8), A("one", 0, 144, 1, 8), [[1, 144]], ALU.is_equal, -15, -16)
+    select("zz", whole("zz"), whole("blk"), [[0, 9], [1, 16]], ALU.is_equal, -15, 0)
+    add("id0", "G", "iota", (whole("id0"), [[-1, 32]], 32, 1), [whole("id0")], [])
+    tt("dm0", whole("dm0"), A("wh", 15, 143), WH, ALU.subtract)
+    tt("dm1", whole("dm1"), whole("dm0"), A("wh", 31, 159), ALU.subtract)
+    tt("dm2", whole("dm2"), whole("dm1"), A("blk", 0, 128), ALU.mult)
+    ts("dm", DM, whole("dm2"), 128.0, None, ALU.mult)
+    ts("nwh", whole("nwh"), WH, -1.0, None, ALU.mult)
+    tt("sh", whole("sh"), WH, A("wh", 0, 128), ALU.add)
+    ts("blkn", whole("blkn"), A("blk", 0, 128), -1.0 / 256, None, ALU.mult)
+    ts("trif", whole("trif"), TRI, 128.0, None, ALU.mult)
+    cp("blkf", whole("blkf"), A("blk", 0, 128))
+    if cfg["zpe"] or "P" in "".join(cfg["acc"]):
+        cp("whf", whole("whf"), WH)
+    ts("id1", whole("id1"), whole("id0"), 15, None, ALU.bitwise_and)
+    ts("idv", whole("idv"), whole("id1"), 0.0, 16.0, ALU.is_equal, ALU.mult)
+    ts("ids", whole("ids"), whole("id1"), 0.0, 128.0, ALU.is_equal, ALU.mult)
+    cp("n16_0", A("n16", 0, C), whole("n0s"))
+    ts("s2k", whole("s2k"), whole("sps"), 1.0 / W, None, ALU.mult)
+
+    def pick(name, eng, out, val, sgn, hot):
+        n = count_of(out)
+        if eng == "V":
+            if not hot:
+                hot.append(A(temp(), 0, n))
+                mm(name + "o", hot[0], [(DM, sgn)])
+            tt(name, out, hot[0], val, ALU.mult)
+        else:
+            b = A(temp(), 0, n)
+            mm(name + "o", b, [(WH, val), (DM, sgn)])
+            act(name, out, b, ACT.Relu, -32768.0, 256.0)
+
+    mark = []
+    for t in range(TK):
+        T_ = "%d" % t
+        no, po, so, mo = t * C, t * R, 2 * t * R, 3 * t * C
+        send("n" + T_, A("nin", no, no + C), A("n16", no, no + C), 1)
+        if t == 1:
+            send("nh", A("nin", 3 * C, 4 * C), A("n16", no, no + C), 2)
+        b = temp()
+        mm("cd" + T_, A(b, 0, 2 * C), [(A("z8", 15 - m, 143 - m, 1, 8), A("uas", 3 * t * R + m, (3 * t + 2) * R, 16, 8))
+                                       for m in range(16)])
+        act("c" + T_, A("cd", no, no + C), A(b, 0, C), ACT.Copy, 0.0, 1.0 / 128)
+        act("d" + T_, A("cd", 3 * C + no, 4 * C + no), A(b, C, 2 * C), ACT.Copy, 0.0, 1.0 / 32768)
+        cut(cfg["chunks"])
+        for j, (a, b) in enumerate(ch):
+            J = T_ + "_%d" % j
+            nj = A("n16", no + a // 16, no + b // 16)
+            q, p = A("q1", a, b), A("pp", po + a, po + b)
+            s1, r = A("s1r", so + a, so + b), A("s1r", so + R + a, so + R + b)
+            gather("gq" + J, cfg["gq"][t][j], q, X(QR, nj))
+            gather("gp" + J, cfg["gp"][t][j], p, X(whole("ptab"), nj))
+            d = A(temp(), 0, b - a)
+            mm("d1a_" + J, d, [(NSEL, A("uds", 2 * t * R + a, 2 * t * R + b, 1, 8))], True, False)
+            mm("d1_" + J, d, [(TRI, q)], False, True)
+            act("s1_" + J, s1, d, ACT.Sign, 0.5, -1.0)
+            hot = []
+            pick("selq" + J, cfg["selq"][t][j], A("sel1", *pair(cfg["ga"], 0, j)), q, s1, hot)
+            pick("selp" + J, cfg["selp"][t][j], A("sel1", *pair(cfg["ga"], 1, j)), p, s1, hot)
+            d = A(temp(), 0, b - a)
+            mm("dr_" + J, d, [(WH, p), (whole("nwh"), q)])
+            act("r_" + J, r, d, ACT.Relu, 0.0, 2.0)
+        if t < TK - 1:
+            send("p" + T_, A("pin", po, po + R), A("pp", po, po + R), 1)
+        for k, grp in enumerate(cfg["gr"]):
+            a, b = span(grp)
+            send("r%d_%d" % (t, k), A("rin", po + a, po + b), A("s1r", so + R + a, so + R + b), 1)
+        for k, grp in enumerate(cfg["ga"]):
+            J = T_ + "_%d" % k
+            a, b = span(grp)
+            ca, cb = a // 16, b // 16
+            n, bk = cb - ca, temp()
+            mm("red1_" + J, A(bk, 0, 2 * n), to_list("sel1", 2 * a, 2 * b))
+            acc = A("msg", mo + ca, mo + cb)
+            tt("a1_" + J, A("t1", ca, cb), A(bk, 0, n), A("cd", no + ca, no + cb), ALU.mult)
+            tt("a2_" + J, acc, A(bk, n, 2 * n), A("t1", ca, cb), ALU.is_gt)
+            if cfg["zpe"] & 1:
+                z = A(temp(), 0, n)
+                mm("a3_" + J, z, [(whole("whf"), A("s2k", no + ca, no + cb)), (WH, acc)])
+                ts("a4_" + J, A("off1", ca, cb), z, 2.0 * W, None, ALU.mult)
+            else:
+                tt("a3_" + J, A("z1", ca, cb), acc, A("s2k", no + ca, no + cb), ALU.add)
+                ts("a4_" + J, A("off1", ca, cb), A("z1", ca, cb), float(W), None, ALU.mult)
+        bk = temp()
+        mm("red1b" + T_, A(bk, 0, 2 * C), to_list("s1r", so, so + 2 * R))
+        act("msg" + T_, A("msg", mo + C, mo + 3 * C), A(bk, 0, 2 * C), ACT.Copy)
+        send("m" + T_, A("mi", mo, mo + 3 * C), A("msg", mo, mo + 3 * C), 1)
+        sc1 = [cp("sc1_%d_%d" % (t, k), X(QW, A("off1", a // 16, b // 16)), A("pp", po + a, po + b))
+               for k, (a, b) in enumerate(pieces(cfg["ga"]))]
+        cut(cfg["chb"])
+        if t == 1:
+            for j, (a, b) in enumerate(ch):
+                act("h1_%d" % j, A("hh", a, b), X(whole("vtab"), A("nin", 3 * C + a // 16, 3 * C + b // 16)), ACT.Tanh)
+        if t == 2:
+            for j, (a, b) in enumerate(ch):
+                vj = X(whole("vtab"), A("nin", no + a // 16, no + b // 16))
+                if cfg["h2"] == "dma":
+                    act("v2_%d" % j, A("v2", a, b), vj, ACT.Copy)
+                else:
+                    tt("v2_%d" % j, A("hs", a, b), vj, A("hh", a, b), ALU.add)
+            if cfg["h2"] == "dma":
+                dma("hadd", "G", whole("hh"), whole("v2"), "hadd", 128 * R * 4, True)
+            for j, (a, b) in enumerate(ch):
+                act("h2_%d" % j, A("hh", a, b), A("hh" if cfg["h2"] == "dma" else "hs", a, b), ACT.Tanh)
+        macc, ms1, mS = A("mi", mo, mo + C), A("mi", mo + C, mo + 2 * C), A("mi", mo + 2 * C, mo + 3 * C)
+        tt("ds" + T_, whole("ds"), mS, A("cd", 3 * C + no, 4 * C + no), ALU.mult)
+        act("ab" + T_, whole("ab"), macc, ACT.Copy, 0.0, 256.0)
+        tt("xx" + T_, whole("xx"), whole("ds"), whole("ab"), ALU.max)
+        if t < TK - 1 and not cfg["zpe"] & 2:
+            tt("zs" + T_, whole("zs"), macc, A("s2k", no, no + C), ALU.add)
+        act("rej" + T_, whole("rej"), macc, ACT.Identity, 1.0, -1.0)
+        tt("aa" + T_, whole("aa"), macc, ms1, ALU.mult)
+        for j, (a, b) in enumerate(ch):
+            J = T_ + "_%d" % j
+            nj = A("nin", no + a // 16, no + b // 16)
+            q, r, n = A("q2", a, b), A("rin", po + a, po + b), b - a
+            s2, s3 = A("s23", *pair(cfg["gb"], 0, j)), A("s23", *pair(cfg["gb"], 1, j))
+            gather("ge" + J, cfg["ge"][t][j], A("ecol", a, b), X(whole("etab"), nj))
+            g2 = gather("gq2" + J, cfg["gq2"][t][j], q, X(QR, nj))
+            if j == 0:
+                mark = [g2]
+            d = A(temp(), 0, n)
+            mm("d2a_" + J, d, [(NSEL, A("uds", (2 * t + 1) * R + a, (2 * t + 1) * R + b, 1, 8))], True, False)
+            mm("d2_" + J, d, [(TRI, q)], False, True)
+            act("s2_" + J, s2, d, ACT.Sign, 0.5, -1.0)
+            hot = []
+            pick("selq2" + J, cfg["selq2"][t][j], A("sel2", *pair(cfg["gb"], 0, j)), q, s2, hot)
+            pick("selr" + J, cfg["selr"][t][j], A("sel2", *pair(cfg["gb"], 1, j)), r, s2, hot)
+            d = A(temp(), 0, n)
+            mm("sb_" + J, d, [(whole("blkn"), r)])
+            how, sq, w = cfg["acc"][t][j], A("sq", a, b), A("ww", a, b)
+            if how == "V":
+                tt("sq_" + J, d, d, q, ALU.mult)
+                tt("dl_" + J, d, d, r, ALU.add)
+                act("w_" + J, w, d, ACT.Relu)
+            elif how == "P":
+                tt("sq_" + J, sq, d, q, ALU.mult)
+                d = A(temp(), 0, n)
+                mm("dl_" + J, d, [(WH, r), (whole("whf"), sq)])
+                act("w_" + J, w, d, ACT.Relu, 0.0, 2.0)
+            else:
+                tt("sq_" + J, sq, d, q, ALU.mult)
+                dma("dl_" + J, "G", sq, r, "dl_" + J, 128 * n * 8, True)
+                act("w_" + J, w, sq, ACT.Relu)
+            d = A(temp(), 0, n)
+            mm("eb_" + J, d, [(NSEL, A("uas", (3 * t + 2) * R + a, (3 * t + 2) * R + b, 1, 8))])
+            tt("ew_" + J, A("ew", a, b), d, w, ALU.mult)
+            d = A(temp(), 0, n)
+            mm("cu_" + J, d, [(whole("trif"), w)], True, False)
+            mm("cv_" + J, d, [(whole("blkf"), A("ew", a, b))], False, True)
+            act("s3_" + J, s3, d, ACT.Sign, 1.0 / 512, -1.0)
+        for k, grp in enumerate(cfg["gb"]):
+            J = T_ + "_%d" % k
+            a, b = span(grp)
+            ca, cb = a // 16, b // 16
+            n, bk = cb - ca, temp()
+            b2, b3 = A("beta", 2 * ca, 2 * ca + n), A("beta", 2 * ca + n, 2 * cb)
+            mm("red2_" + J, A(bk, 0, 2 * n), to_list("sel2", 2 * a, 2 * b))
+            tt("b1_" + J, A("t2", ca, cb), A(bk, 0, n), A("xx", ca, cb), ALU.mult)
+            tt("b2_" + J, b2, A(bk, n, 2 * n), A("t2", ca, cb), ALU.is_gt)
+            tt("b5_" + J, b3, A("rej", ca, cb), b2, ALU.subtract)
+            if t < TK - 1 and cfg["zpe"] & 2:
+                z = A(temp(), 0, n)
+                mm("b3_" + J, z, [(whole("whf"), A("s2k", no + ca, no + cb)), (WH, A("mi", mo + ca, mo + cb)), (WH, b2)])
+                ts("b4_" + J, A("off2", ca, cb), z, 2.0 * W, None, ALU.mult)
+            elif t < TK - 1:
+                tt("b3_" + J, A("z2", ca, cb), b2, A("zs", ca, cb), ALU.add)
+                ts("b4_" + J, A("off2", ca, cb), A("z2", ca, cb), float(W), None, ALU.mult)
+            bk = temp()
+            mm("red3_" + J, A(bk, 0, 2 * n), to_list("s23", 2 * a, 2 * b))
+            tt("c1_" + J, A("prod", 2 * ca, 2 * cb), A(bk, 0, 2 * n), A("beta", 2 * ca, 2 * cb), ALU.mult)
+            three = [A("aa", ca, cb), A("prod", 2 * ca, 2 * ca + n), A("prod", 2 * ca + n, 2 * cb)]
+            bk = temp()
+            mm("kk_" + J, A(bk, 0, n), [(whole("sh"), x) for x in three])
+            ts("c2_" + J, A("k16", ca, cb), A(bk, 0, n), A("kc", 0, 1), None, ALU.add)
+            for j in grp:
+                a1, b1 = ch[j]
+                J1 = T_ + "_%d" % j
+                kj, e = A("k16", a1 // 16, b1 // 16), A("ecol", a1, b1)
+                if cfg["sele"][t][j] == "V":
+                    tt("sele" + J1, A("sele", a1, b1), X(whole("idv"), kj), e, ALU.mult)
+                else:
+                    act("hot" + J1, A("hot", a1, b1), X(whole("ids"), kj), ACT.Copy)
+                    d = A(temp(), 0, b1 - a1)
+                    mm("de_" + J1, d, [(WH, e), (WH, A("hot", a1, b1))])
+                    act("sele" + J1, A("sele", a1, b1), d, ACT.Relu, -2048.0, 32.0)
+            bk = temp()
+            mm("nn_" + J, A(bk, 0, n), [(WH, x) for x in three] + to_list("sele", a, b))
+            ts("c3_" + J, A("n16", no + C + ca, no + C + cb), A(bk, 0, n), 8.0, None, ALU.add)
+            act("nf" + J, A("nf", no + ca, no + cb), A(bk, 0, n), ACT.Identity, 8.0)
+        if t < TK - 1:
+            for k, (a, b) in enumerate(pieces(cfg["gb"])):
+                cp("sc2_%d_%d" % (t, k), X(QW, A("off2", a // 16, b // 16)), A("pin", po + a, po + b))
+    dma("st_n", "Y", D("yn"), whole("nf"), "st", 128 * C * 12)
+    for j, (a, b) in enumerate(ch):
+        tt("v3_%d" % j, A("hs", a, b), X(whole("vtab"), A("n16", 3 * C + a // 16, 3 * C + b // 16)), A("hh", a, b), ALU.add)
+        act("h3_%d" % j, A("ho", a, b), A("hs", a, b), ACT.Tanh)
+        dma("st_h%d" % j, "Y", D("yh", a, b), A("ho", a, b), "st", 128 * (b - a) * 4)
+    return ops
+
+
+def plan(cfg, m=None):
+    ops = graph(cfg)
+    order, bank_of, end, holder, users = cfg.get("order", list(range(len(ops)))), {}, 0.0, {}, {}
+    if isinstance(order, str):
+        order = [DIGITS.index(order[k]) * 32 + DIGITS.index(order[k + 1]) for k in range(0, len(order), 2)]
+    for o in ops:
+        for tp in o["temps"]:
+            users.setdefault(tp, []).append(o["i"])
+    for i in order:
+        for tp in ops[i]["temps"]:
+            if tp not in bank_of:
+                bk = int(cfg["banks"][len(bank_of)]) if "banks" in cfg else len(bank_of) % 8
+                bank_of[tp] = bk
+                ops[i]["deps"] = ops[i]["deps"] | set(users.get(holder.get(bk), []))
+                holder[bk] = tp
+    pos, know, clock, need, cnt = {}, {}, {}, set(), {}
+    for i in order:
+        o = ops[i]
+        e = o["eng"]
+        k = know.setdefault(e, {})
+        o["waits"] = []
+        for d in sorted(o["deps"], key=lambda x: -pos[x][2]):
+            line, at = pos[d][0], pos[d][1]
+            if k.get(line, -1) >= at:
+                continue
+            o["waits"].append(d)
+            need.add(d)
+            for l2, a2 in clock[d].items():
+                k[l2] = max(k.get(l2, -1), a2)
+        line = e if o["kind"] == "c" else o["sem"]
+        if o["kind"] == "dma":
+            o["val"] = 16 * sum(1 for x in ops if x.get("sem") == o["sem"])
+        cnt[line] = cnt.get(line, -1) + 1
+        pos[i] = (line, cnt[line], len(pos))
+        clock[i] = {} if o["kind"] == "send" else dict(k)
+        clock[i][line] = cnt[line]
+    total = {}
+    for i in order:
+        o = ops[i]
+        o["inc"] = o["kind"] != "c" or i in need
+        if o["kind"] == "c" and o["inc"]:
+            total[o["eng"]] = total.get(o["eng"], 0) + 1
+            o["val"] = total[o["eng"]]
+    return {"ops": ops, "order": order, "bank": bank_of, "end": end, "total": total}
+
+
+PLAN = plan(CFG)
+SEMAPHORES = ["eV", "eS", "eP", "eG", "sent"] + sorted({o["sem"] for o in PLAN["ops"] if o["kind"] != "c"})
+
+
+def rank_program(g, core, T, topo):
+    rank = T.rank_of(core)
+    if rank is None:
+        return
+    ops, N = PLAN["ops"], len(T.cores)
+    queue = {"G": g, "V": g.vector, "S": g.scalar, "P": g.tensor, "Y": g.sync}
+
+    def ap(x):
+        if not isinstance(x, tuple):
+            return x
+        if x[0] == "ind":
+            return ap(x[1]).indirect(ap(x[2]))
+        if x[0] == "dram":
+            return T[x[1]][:] if x[2] is None else T[x[1]][:, x[2]:x[3]]
+        name = "bank%d" % PLAN["bank"][x[1]] if x[1][0] == "@" else x[1]
+        if isinstance(x[5], tuple):
+            return T[name][x[5][0]:x[5][1]:x[5][2], x[2]:x[3]]
+        if x[4] == 1:
+            return T[name][0:x[5], x[2]:x[3]]
+        return T[name][0:x[5], x[2]:x[3]:x[4]]
+
+    def arrivals(hop):
+        return len(topo.engines(T.cores[(rank - hop) % N], core))
+
+    sent, stores = [0], [0]
+    for i in PLAN["order"]:
+        o = ops[i]
+        q, c, a = queue[o["eng"]], o["call"], o["args"]
+        for d in o["waits"]:
+            od = ops[d]
+            if od["kind"] == "c":
+                q.wait_ge(T.sem["e" + od["eng"]], od["val"])
+            else:
+                q.wait_ge(T.sem[od["sem"]], od["val"] if od["kind"] == "dma" else arrivals(od["args"][2]))
+        if c == "send":
+            dst = T.cores[(rank + a[2]) % N]
+            rid, pid, _se = topo.addr(dst)
+            g.remote_dma(ap(a[0]), ap(a[1]), T.sem[o["sem"]], T.sem["sent"], pid, rid, topo.mask(core, dst))
+            sent[0] += len(topo.engines(core, dst))
+            continue
+        if c == "dma":
+            ins = q.dma_start(ap(a[0]), ap(a[1]), accum_op=ALU.add) if a[2] else q.dma_start(ap(a[0]), ap(a[1]))
+            ins.then_inc(T.sem[o["sem"]], 16)
+            stores[0] += 16 if o["sem"] == "st" else 0
+            continue
+        if c == "mm":
+            for k, (x, y) in enumerate(a[1]):
+                ins = q.matmul(ap(a[0]), ap(x), ap(y), a[2] and k == 0, a[3] and k == len(a[1]) - 1)
+        elif c == "tt":
+            ins = q.tensor_tensor(ap(a[0]), ap(a[1]), ap(a[2]), a[3])
+        elif c == "ts":
+            if a[5] is None:
+                ins = q.tensor_scalar(ap(a[0]), ap(a[1]), ap(a[2]), None, a[4])
+            else:
+                ins = q.tensor_scalar(ap(a[0]), ap(a[1]), ap(a[2]), ap(a[3]), a[4], a[5])
+        elif c == "cp":
+            ins = q.tensor_copy(ap(a[0]), ap(a[1]))
+        elif c == "act":
+            ins = q.activation(ap(a[0]), ap(a[1]), a[2], bias=a[3], scale=a[4])
+        elif c == "fill":
+            ins = q.memset(ap(a[0]), a[1])
+        elif c == "sel":
+            ins = q.affine_select(ap(a[0]), ap(a[1]), a[2], a[3], 0.0, a[4], a[5])
+        else:
+            ins = q.iota(ap(a[0]), a[1], a[2], a[3])
+        if o["inc"]:
+            ins.then_inc(T.sem["e" + o["eng"]], 1)
+    for e, v in PLAN["total"].items():
+        g.wait_ge(T.sem["e" + e], v)
+    g.wait_ge(T.sem["sent"], sent[0])
+    g.sync.wait_ge(T.sem["st"], stores[0])

@@ -1,34 +1,39 @@
+import math
+import numpy as np
 from concourse.bass import DstId, RemoteDMATransfer
 from concourse.mybir import AluOpType, ActivationFunctionType
 
 ALU = AluOpType
 ACT = ActivationFunctionType
 R, W, TK, C = 1536, 2048, 3, 96
-DIGITS = "0123456789abcdefghijklmnopqrstuv"
 
 CFG = {
-    "chunks": [512, 512, 512], "chb": [512, 512, 512],
-    "ga":[[0],[1,2]],"gb":[[0],[1],[2]],"gr":[[0],[1,2]],"gq":["SVV","SVS","SVV"],"gp":["VSV","VSS","SSV"],"gq2":["SVS","SVS","SVS"],"ge":["SSS","SSS","SSS"],"selq":["VSS","VVS","VVS"],"selp":["SVS","VVV","VSS"],"selq2":["VVV","VVS","VVV"],"selr":["VSV","VSS","VVV"],"sele":["SSV","SSV","VVV"],"h2":"dma","acc":["VVV","VVV","VVV"],"loads":"ndaqpseADv","zpe":0,"piece":1024,
-    "order":"0b000c0j0n0o010a020i030f0g0k0p0s0h21040506070809131b0d0l0r160t0u150v0q1m17183e191k1n1v1c1o0e1d0m10221p231a1r1e1l1f1g201i1h241q1s2d2514261j2e2f2g1t272h2b2q283j2i1u292j2k2c2n2l2m2r40452o472p4h3a2a343l11333k463b3m353s3c363t3d374812303u3g493f3v4a383n3h4c2t393o3i4d4b3q2s4m3r3p41325m4e2u4s564f4n4g5n4o42312v5o4q4j4p575p584t4i435a594r5q644k444u4l5c4v5b505s5d655e51695f5r5g5t665u525h5v6a535i6b5j54606c6e5k6o6m6n6f616d6g6p6h6q626k6j68706r676i72716s737e6t746u7f7g63777h6v7i75787r79767a7j6l7d7t7c9b7k7o7l7m7n7s94887p86bd7q7b7v558ibf5l8o9a9i908p87919c8q9j9d89928a8e8f938b8c8r968d84958s8u8g979k8h808v8t98838jbe9r818n7u82ab9s8k859l9t9v9g9uaca0ad9eb98l9m8m9o9n99afagaea19f9pa2a3ahba9h9qara4a5b1asaiatauajavbsakb0c7alb2bba6b3a7ama8anb4aoa9b5bgbiapb6bhbqbjaab7bobkbcc5brblbtbnc8bpc3bmbucgc6cic9bvcjc4c1ckc0cac2clcmcccvcbcecdcfcnd3chehcoaqd2cscpcqcrd0ercte0b8cud1dfdldpd4dedvenegdme1dgdne2eie6eodoe3epdbdrejdqeqe7ekdhetesemdid5dsdjddefdkeuele5f0d8evdce8dteafoe4d9e9f4dudaebfsd6f1ecfpf2fqf3d7frf5ftf6fcf7f8fuedfvfdg0f9eefefgfaffg5g1fhg6fig2fjg3g7fkgbflgcfmg8fbgdfng4g9ga",
-    "banks":"0123456723107256103725615234165236405126374501623547625762357624370152012652104365724061357204375247561427561402531072546572013645721",
+    "chunks": [[512, 512, 512]] * 3, "sele": ["SVV", "SVV", "VVV"], "dsend": [512, 512, 512],
+    "split": ["row", "nn"], "early": ["---", "bb-", "---", "bb-", "---", "bb-"],
+    "loads": "nq0psadev", "slack": 60.0, "steps": 130000, "seed": 1,
 }
 
 BF, F32, I32, U16 = "bfloat16", "float32", "int32", "uint16"
 SB = {
-    "qw": (BF, 2 * W), "ptab": (BF, W), "etab": (BF, W), "vtab": (BF, W), "uds": (BF, 6 * R), "uas": (BF, 9 * R),
-    "n0s": (I32, C), "sps": (I32, 3 * C), "s2k": (F32, 3 * C), "cd": (F32, 6 * C),
+    "qw": (BF, 2 * W), "ptab": (BF, W), "etab": (BF, W), "vtab": (BF, W), "uds": (BF, R), "uas": (BF, R),
+    "n0s": (I32, C), "sps": (I32, 3 * C), "sph": (BF, 3 * C), "spl": (BF, 3 * C), "cd": (F32, 9 * C),
+    "ec": (F32, C), "th": (I32, C), "hl": (BF, 2 * C), "rt": (BF, 768), "selb0": (BF, 512), "selb": (BF, 512),
     "n16": (U16, 4 * C), "nin": (U16, 4 * C), "off1": (U16, C), "off2": (U16, C), "k16": (U16, C),
-    "q1": (BF, R), "q2": (BF, R), "ecol": (BF, R), "hot": (BF, R), "sele": (BF, R), "v2": (BF, R),
-    "sel1": (BF, 2 * R), "sel2": (BF, 2 * R), "s23": (BF, 2 * R), "pp": (BF, 3 * R), "s1r": (BF, 6 * R),
-    "rin": (BF, 3 * R), "pin": (BF, 2 * R), "msg": (BF, 9 * C), "mi": (BF, 9 * C),
-    "ww": (F32, R), "ew": (F32, R), "sq": (F32, R), "hh": (F32, R), "hs": (F32, R), "ho": (F32, R),
-    "t1": (F32, C), "z1": (F32, C), "t2": (F32, C), "z2": (F32, C), "ds": (F32, C), "ab": (F32, C), "xx": (F32, C),
-    "zs": (F32, C), "rej": (F32, C), "aa": (BF, C), "beta": (BF, 2 * C), "prod": (BF, 2 * C), "nf": (F32, 3 * C),
-    "one": (BF, 160), "half": (BF, 160), "neg": (BF, 128), "blk0": (BF, 144), "blk": (BF, 144), "tri": (BF, 128),
-    "zz": (BF, 144), "z8": (BF, 144), "nsel": (BF, 128), "wh": (BF, 160), "nwh": (BF, 128), "dm0": (BF, 128),
-    "dm1": (BF, 128), "dm2": (BF, 128), "dm": (BF, 128), "sh": (BF, 128), "blkn": (BF, 128), "trif": (F32, 128),
-    "blkf": (F32, 128), "whf": (F32, 128), "id0": (I32, 32), "id1": (I32, 32), "idv": (BF, 32), "ids": (BF, 32),
-    "kc": (F32, 4),
+    "q1": (BF, 3 * R), "pp": (BF, 3 * R), "din": (BF, 3 * R), "pin": (BF, 2 * R), "rin": (BF, R),
+    "q2": (BF, R), "ecol": (BF, R), "hot": (BF, R), "sele": (BF, R), "v2": (BF, R), "s3": (BF, R),
+    "st1": (BF, R), "st2": (BF, R), "sc1": (F32, R), "sc2": (F32, R),
+    "ww": (F32, R), "hh": (F32, R), "hs": (F32, R), "ho": (F32, R),
+    "msg": (BF, 6 * C), "mi": (BF, 6 * C), "ds": (F32, C), "ud0": (BF, R),
+    "li1": (I32, C), "qi1": (I32, C), "lo1": (I32, C), "tb1": (F32, C), "y1": (BF, C),
+    "li2": (I32, C), "qi2": (I32, C), "lo2": (I32, C), "tb2": (F32, C), "y2": (BF, C),
+    "ab": (F32, C), "xx": (F32, C), "bp": (BF, 2 * C),
+    "nf": (F32, 3 * C), "ra": (BF, 768), "rb": (BF, 768), "rv": (BF, 768),
+    "one": (BF, 640), "blk0": (BF, 144), "blk": (BF, 144), "zz": (BF, 144), "idn": (BF, 128), "tris": (BF, 128),
+    "tri": (BF, 128), "ntrif": (F32, 128), "b8f": (F32, 8), "blkn": (BF, 128), "n143": (BF, 128),
+    "nbig": (BF, 128), "zer": (BF, 512),
+    "y4": (BF, 128), "m0": (BF, 128), "m1": (BF, 128), "pk": (BF, 128), "i20": (BF, 128),
+    "h0": (BF, 8), "h1": (BF, 8), "hb": (BF, 56), "rl": (BF, 144), "rk": (BF, 144), "nsu": (BF, 768),
+    "selt": (BF, 72), "id0": (I32, 32), "id1": (I32, 32), "idv": (BF, 32), "ids": (BF, 32),
 }
 SIZE = {BF: 2, F32: 4, I32: 4, U16: 2}
 SCRATCH = {k: ("sbuf", [128, v[1]], v[0]) for k, v in SB.items()}
@@ -69,7 +74,7 @@ def graph(cfg):
 
     def add(name, eng, call, args, outs, ins, soft=(), **kw):
         i = len(ops)
-        deps, acc = set(), []
+        deps, reads, acc = set(), set(), []
         for o in outs:
             ps = parts_of(o)
             acc += [(ps[0], True)] + [(p, False) for p in ps[1:]] if ps else []
@@ -77,23 +82,24 @@ def graph(cfg):
             acc += [(p, False) for p in parts_of(o)]
         for p, wr in acc:
             bank = p[1][0] == "@"
-            for (a, b, j, w2, rows) in seen.get(p[1], []):
-                if bank:
-                    if wr or w2 or ops[j]["eng"] != eng:
-                        deps.add(j)
-                elif a < p[3] and p[2] < b and (wr or w2) and not (isinstance(rows, tuple) and isinstance(p[5], tuple)):
+            for (a, b, j, w2) in seen.get(p[1], []):
+                if (wr or w2 or ops[j]["eng"] != eng) if bank else (a < p[3] and p[2] < b and (wr or w2)):
                     deps.add(j)
+                    if w2 and not (wr and eng == "P"):
+                        reads.add(j)
         for p, wr in acc:
-            seen.setdefault(p[1], []).append((p[2], p[3], i, wr, p[5]))
+            seen.setdefault(p[1], []).append((p[2], p[3], i, wr))
         deps.discard(i)
-        op = {"i": i, "name": name, "eng": eng, "call": call, "args": args, "deps": deps, "soft": set(soft),
-              "temps": sorted({p[1] for p, _w in acc if p[1][0] == "@"}), "kind": "c"}
+        op = {"i": i, "name": name, "eng": eng, "call": call, "args": args, "deps": deps, "reads": reads,
+              "soft": set(soft), "temps": sorted({p[1] for p, _w in acc if p[1][0] == "@"}), "kind": "c"}
         op.update(kw)
         ops.append(op)
         return i
 
-    def mm(name, out, terms, start=True, stop=True, soft=()):
-        return add(name, "P", "mm", (out, terms, start, stop), [out], [x for t in terms for x in t], soft)
+    def mm(name, sums, start=True, stop=True, soft=()):
+        calls = [(o, x, y, start and k == 0, stop and k == len(terms) - 1)
+                 for o, terms in sums for k, (x, y) in enumerate(terms)]
+        return add(name, "P", "mm", calls, [c[0] for c in calls], [x for c in calls for x in c[1:3]], soft)
 
     def tt(name, out, a, b, op):
         return add(name, "V", "tt", (out, a, b, op), [out], [a, b])
@@ -104,11 +110,14 @@ def graph(cfg):
     def cp(name, out, a):
         return add(name, "V", "cp", (out, a), [out], [a])
 
+    def scan(name, out, a, b):
+        return add(name, "V", "scan", (out, a, b), [out], [a, b])
+
     def act(name, out, a, func, bias=0.0, scale=1.0):
         return add(name, "S", "act", (out, a, func, bias, scale), [out], [a])
 
-    def gather(name, eng, out, a):
-        return cp(name, out, a) if eng == "V" else act(name, out, a, ACT.Copy)
+    def either(name, eng, out, a, scale=1.0, relu=False):
+        return add(name, eng, "either", (out, a, scale, relu), [out], [a])
 
     def fill(name, out, v):
         return add(name, "V", "fill", (out, v), [out], [])
@@ -116,281 +125,466 @@ def graph(cfg):
     def select(name, out, a, pat, op, base, cm):
         return add(name, "G", "sel", (out, a, pat, op, base, cm), [out], [a])
 
+    def iota(name, out, pat, base, cm):
+        return add(name, "G", "iota", (out, pat, base, cm), [out], [])
+
     def dma(name, eng, out, a, sem, nbytes, accum=False, soft=()):
         return add(name, eng, "dma", (out, a, accum), [out], [a] + ([out] if accum else []), soft, kind="dma", sem=sem,
                    nbytes=nbytes)
 
-    def send(name, out, a, hop):
-        return add(name, "G", "send", (out, a, hop), [out], [a], kind="send", sem=name,
-                   nbytes=128 * count_of(a) * SIZE[SB[a[1]][0]])
+    def send(name, out, srcs, hop, alu=0):
+        return add(name, "G", "send", (out, srcs, hop, alu), [out], srcs, kind="send", sem=name,
+                   nbytes=128 * count_of(out) * SIZE[SB[out[1]][0]])
 
     def whole(n, rows=128):
         return A(n, 0, SB[n][1], 1, rows)
 
-    ch = []
-
     def cut(sizes):
-        ch[:] = [(sum(sizes[:k]), sum(sizes[:k + 1])) for k in range(len(sizes))]
+        return [(sum(sizes[:k]), sum(sizes[:k + 1]), k) for k in range(len(sizes))]
 
-    def span(grp):
-        return ch[grp[0]][0], ch[grp[-1]][1]
+    def wide(buf, ch, at=0):
+        return A(buf, at + ch[0], at + ch[1])
 
-    def pair(groups, which, j):
-        for grp in groups:
-            if j in grp:
-                a, b = span(grp)
-                o = 2 * a + which * (b - a) + ch[j][0] - a
-                return o, o + ch[j][1] - ch[j][0]
+    def small(buf, ch, at=0):
+        return A(buf, at + ch[0] // 16, at + ch[1] // 16)
 
-    def pieces(groups):
-        out = []
-        for grp in groups:
-            a, b = span(grp)
-            out += [(x, min(b, x + cfg["piece"])) for x in range(a, b, cfg["piece"])]
+    def pair(buf, ch, at=0, k=None):
+        return A(buf, at + ch[0] // 8 + (k or 0), at + ch[1] // 8, 1 if k is None else 2)
+
+    def blocks(buf, ch, at=0, rows=128):
+        nb = (ch[1] - ch[0]) // 128
+        return [A(buf, at + ch[0] + b, at + ch[1], nb, rows) for b in range(nb)]
+
+    def turned(name, chs, width, terms, soft=()):
+        bk, sums = temp(), []
+        for ch in chs:
+            for b in range((ch[1] - ch[0]) // 128):
+                at = width * len(sums)
+                sums.append((A(bk, at, at + width), [(blocks(x, ch, o, rows)[b], y) for x, o, rows, y in terms]))
+        return A(bk, 0, width * len(sums)), mm(name, sums, soft=soft)
+
+    def turned_early(name, ch, early, late, soft=()):
+        bk, nb = temp(), (ch[1] - ch[0]) // 128
+        out = A(bk, 0, 128 * nb)
+        for tag, (x, o, rows, y) in (("a", early), ("", late)):
+            calls = [(A(bk, 128 * b, 128 * b + 128), blocks(x, ch, o, rows)[b], y, False, not tag and b == nb - 1)
+                     for b in range(nb)]
+            if tag:
+                calls.insert(0, (out, A("zer", 0, 128, 1, 32), A("zer", 0, 128 * nb, 1, 32), True, False))
+            m = add(name + tag, "P", "mm", calls, [out], [v for c in calls for v in c[1:3]], () if tag else soft)
+        return out, m
+
+    def summed(name, out, early, late):
+        if early and name.rstrip("0123456789_l") in cfg["split"]:
+            mm(name + "a", [(out, early)], True, False)
+            mm(name, [(out, late)], False)
+        else:
+            mm(name, [(out, early + late)])
         return out
 
-    def to_list(buf, a, b):
-        return [(A("zz", 15 - m, 143 - m), A(buf, a + m, b, 16)) for m in range(16)]
+    def to_rows(name, ch, early, late):
+        return summed(name, A(temp(), 0, 128, 1, (ch[1] - ch[0]) // 16), early, late)
 
-    WH, QW, QR = A("wh", 16, 144), whole("qw"), A("qw", 0, W)
-    TRI, NSEL, DM = whole("tri"), whole("nsel", 8), whole("dm")
+    def rows_of(buf, ch):
+        return A(buf, 128 * ch[2], 128 * ch[2] + 128, 1, (ch[1] - ch[0]) // 16)
+
+    def from_rows(mat, buf, ch):
+        nb = (ch[1] - ch[0]) // 128
+        return [(A(mat, 16 - nb * u, 144 - nb * u, 1, 8 * nb),
+                 A(buf, 128 * ch[2] + u, 128 * ch[2] + 128, 16 // nb, 8 * nb)) for u in range(16 // nb)]
+
+    def to_list(name, ch, early, late):
+        return summed(name, A(temp(), 0, (ch[1] - ch[0]) // 16), early, late)
+
+    def offsets(name, out, rows, buf, ch, t):
+        act(name + "r", rows_of(buf, ch), rows, ACT.Copy, 0.0, float(W))
+        cp(name, small(out, ch), to_list(name + "l", ch, [(IDN, small(s, ch, t * C)) for s in ("sph", "spl")],
+                                         from_rows("rl", buf, ch)))
+
+    def draft(J, q, low, ilow, at, kind, ch, st, sc):
+        how = cfg["early"][kind][ch[2]]
+        x, y = (q, at, 128, TRIS), ("uds", 0, 48, A("nsu", 128 * kind, 128 * kind + 128, 1, 48))
+        if kind == 0:
+            y = ("ud0", 0, 8, A("nsu", 0, 128, 1, 8))
+        u, m = turned_early("cum" + J, ch, y, x) if how in "ub" else turned("cum" + J, [ch], 128, [x, y])
+        act("st" + J, wide(st, ch), u, ACT.Sign, -0.5, -1.0)
+        x, y = (q, at, 128, whole("pk")), (low, at, 128, whole(ilow))
+        v, m = turned_early("pk" + J, ch, y, x, [m]) if how in "rb" else turned("pk" + J, [ch], 128, [x, y], [m])
+        scan("sc" + J, wide(sc, ch), wide(st, ch), v)
+        return A(sc, ch[0] + 15, ch[1], 16)
+
+    def test(J, L, k, factor, yes, token, ch):
+        li, q, low, bound, y = [small(x + k, ch) for x in ("li", "qi", "lo", "tb", "y")]
+        ts("li" + J, li, L, 2.0 ** 20, None, ALU.mult)
+        ts("q" + J, q, li, 10, 1023, ALU.logical_shift_right, ALU.bitwise_and)
+        ts("r" + J, low, li, 1023, None, ALU.bitwise_and)
+        tt("t" + J, bound, q, factor, ALU.mult)
+        tt("yes" + J, yes, low, bound, ALU.is_gt)
+        act("y" + J, y, L, ACT.Identity, 128.0)
+        tt("tok" + J, token, y, yes, ALU.mult)
+
+    QW, QR, IDN, TRIS = whole("qw"), A("qw", 0, W), whole("idn"), whole("tris")
+    BLK, B8 = A("blk", 0, 128), A("blk", 0, 128, 16)
+    thirds = cut([512, 512, 512])
 
     loads = {"n": (whole("n0s"), D("n0"), 128 * C * 4), "q": (QR, D("qd"), 128 * W * 2),
-             "p": (whole("ptab"), D("pt"), 128 * W * 2), "d": (A("uds", 0, 2 * R, 1, 8), D("ud", 0, 2 * R), 8 * 4 * R),
-             "D": (A("uds", 2 * R, 6 * R, 1, 8), D("ud", 2 * R, 6 * R), 8 * 8 * R),
-             "a": (A("uas", 0, 3 * R, 1, 8), D("ua", 0, 3 * R), 8 * 6 * R),
-             "A": (A("uas", 3 * R, 9 * R, 1, 8), D("ua", 3 * R, 9 * R), 8 * 12 * R),
-             "s": (whole("sps"), D("spot"), 128 * C * 12),
+             "p": (whole("ptab"), D("pt"), 128 * W * 2), "d": (whole("uds", 48), D("ud"), 48 * R * 2),
+             "0": (whole("ud0", 8), D("ud", 0, R), 8 * R * 2),
+             "a": (whole("uas", 72), D("ua"), 72 * R * 2), "s": (whole("sps"), D("spot"), 128 * C * 12),
              "e": (whole("etab"), D("nx"), 128 * W * 2), "v": (whole("vtab"), D("vf"), 128 * W * 2)}
     prev = []
     for k in cfg["loads"]:
-        prev = [dma("ld_" + k, "Y", loads[k][0], loads[k][1], "ld%d" % ord(k), loads[k][2], soft=prev)]
+        prev = [dma("ld_" + k, "Y", loads[k][0], loads[k][1], "ld_" + k, loads[k][2], soft=prev)]
     fill("one", whole("one"), 1.0)
-    fill("neg", whole("neg"), -1.0)
-    fill("half", whole("half"), 0.5)
-    fill("kc0", whole("kc"), 16.0)
-    fill("kc1", whole("kc", 16), 8.0)
+    fill("zer", whole("zer", 32), 0.0)
     select("blk0", whole("blk0"), A("one", 0, 144), [[-16, 9], [0, 16]], ALU.is_ge, 0, 1)
     select("blk", whole("blk"), whole("blk0"), [[16, 9], [0, 16]], ALU.is_ge, 15, -1)
-    select("tri", TRI, A("blk", 0, 128), [[1, 128]], ALU.is_ge, 0, -1)
-    select("nsel", NSEL, whole("neg", 8), [[1, 8], [0, 16]], ALU.is_equal, 0, -1)
-    select("wh", whole("wh"), whole("half"), [[1, 160]], ALU.is_equal, -16, -1)
-    select("z8", whole("z8", 8), A("one", 0, 144, 1, 8), [[1, 144]], ALU.is_equal, -15, -16)
+    select("tris", TRIS, BLK, [[1, 128]], ALU.is_ge, -1, -1)
+    select("nsu0", A("nsu", 0, 128, 1, 8), A("one", 0, 128, 1, 8), [[-1, 8], [0, 16]], ALU.is_equal, 0, 1)
+    select("idn", IDN, A("one", 0, 128), [[-1, 128]], ALU.is_equal, 0, 1)
+    iota("y4", whole("y4"), [[0, 8], [-4, 16]], 60, 0)
+    select("selt", whole("selt", 72), A("one", 0, 72, 1, 72), [[-1, 9], [-9, 8]], ALU.is_equal, 0, 1)
+    fill("rl0", A("rl", 0, 16, 1, 32), 0.0)
+    select("rl", A("rl", 16, 144, 1, 32), A("one", 0, 128, 1, 32), [[-1, 8], [100, 4], [-8, 4]], ALU.is_equal, 0, 1)
+    select("nsu1", A("nsu", 128, 768, 1, 48), whole("one", 48), [[-1, 5], [-6, 8], [0, 16]], ALU.is_equal, -1, 1)
+    select("selb0", whole("selb0", 64), A("one", 0, 512, 1, 64), [[-16, 4], [-2, 8], [0, 16]], ALU.is_ge, 0, 1)
+    select("selb", whole("selb", 64), whole("selb0", 64), [[16, 4], [2, 8], [0, 16]], ALU.is_ge, 1, -1)
     select("zz", whole("zz"), whole("blk"), [[0, 9], [1, 16]], ALU.is_equal, -15, 0)
-    add("id0", "G", "iota", (whole("id0"), [[-1, 32]], 32, 1), [whole("id0")], [])
-    tt("dm0", whole("dm0"), A("wh", 15, 143), WH, ALU.subtract)
-    tt("dm1", whole("dm1"), whole("dm0"), A("wh", 31, 159), ALU.subtract)
-    tt("dm2", whole("dm2"), whole("dm1"), A("blk", 0, 128), ALU.mult)
-    ts("dm", DM, whole("dm2"), 128.0, None, ALU.mult)
-    ts("nwh", whole("nwh"), WH, -1.0, None, ALU.mult)
-    tt("sh", whole("sh"), WH, A("wh", 0, 128), ALU.add)
-    ts("blkn", whole("blkn"), A("blk", 0, 128), -1.0 / 256, None, ALU.mult)
-    ts("trif", whole("trif"), TRI, 128.0, None, ALU.mult)
-    cp("blkf", whole("blkf"), A("blk", 0, 128))
-    if cfg["zpe"] or "P" in "".join(cfg["acc"]):
-        cp("whf", whole("whf"), WH)
+    iota("id0", whole("id0"), [[-1, 32]], 32, 1)
+    tt("m0", whole("m0"), whole("y4"), BLK, ALU.mult)
+    tt("m1", whole("m1"), whole("m0"), IDN, ALU.add)
+    ts("pk", whole("pk"), whole("m1"), -2.0 ** -10, None, ALU.mult)
+    either("i20", "S", whole("i20"), IDN, 2.0 ** -20)
+    either("n143", "S", whole("n143"), IDN, -143.0)
+    either("nbig", "S", whole("nbig"), IDN, -2.0 ** 17)
+    tt("tri", whole("tri"), TRIS, IDN, ALU.add)
+    either("ntrif", "S", whole("ntrif"), whole("tri"), -1.0)
+    either("blkn", "S", whole("blkn"), BLK, -1.0 / 256)
+    either("b8f", "S", whole("b8f"), B8)
+    ts("h0", whole("h0"), A("idn", 15, 128, 16), 14.0, None, ALU.mult)
+    tt("h1", whole("h1"), whole("h0"), B8, ALU.add)
+    fill("hb0", whole("hb"), 0.0)
+    ts("hb", A("hb", 24, 32), whole("h1"), -0.5, None, ALU.mult)
+    fill("rk0", A("rk", 0, 16, 1, 32), 0.0)
+    tt("rk1", A("rk", 16, 144, 1, 32), A("rl", 16, 144, 1, 32), A("rl", 0, 128, 1, 32), ALU.add)
     ts("id1", whole("id1"), whole("id0"), 15, None, ALU.bitwise_and)
     ts("idv", whole("idv"), whole("id1"), 0.0, 16.0, ALU.is_equal, ALU.mult)
     ts("ids", whole("ids"), whole("id1"), 0.0, 128.0, ALU.is_equal, ALU.mult)
     cp("n16_0", A("n16", 0, C), whole("n0s"))
-    ts("s2k", whole("s2k"), whole("sps"), 1.0 / W, None, ALU.mult)
 
-    def pick(name, eng, out, val, sgn, hot):
-        n = count_of(out)
-        if eng == "V":
-            if not hot:
-                hot.append(A(temp(), 0, n))
-                mm(name + "o", hot[0], [(DM, sgn)])
-            tt(name, out, hot[0], val, ALU.mult)
-        else:
-            b = A(temp(), 0, n)
-            mm(name + "o", b, [(WH, val), (DM, sgn)])
-            act(name, out, b, ACT.Relu, -32768.0, 256.0)
-
-    mark = []
     for t in range(TK):
-        T_ = "%d" % t
-        no, po, so, mo = t * C, t * R, 2 * t * R, 3 * t * C
-        send("n" + T_, A("nin", no, no + C), A("n16", no, no + C), 1)
+        T_, chs = "%d" % t, cut(cfg["chunks"][t])
+        no, po, mo = t * C, t * R, 2 * t * C
+        cp("sph" + T_, A("sph", no, no + C), A("sps", no, no + C))
+        tt("spl" + T_, A("spl", no, no + C), A("sps", no, no + C), A("sph", no, no + C), ALU.subtract)
+        send("n" + T_, A("nin", no, no + C), [A("n16", no, no + C)], 1)
         if t == 1:
-            send("nh", A("nin", 3 * C, 4 * C), A("n16", no, no + C), 2)
-        b = temp()
-        mm("cd" + T_, A(b, 0, 2 * C), [(A("z8", 15 - m, 143 - m, 1, 8), A("uas", 3 * t * R + m, (3 * t + 2) * R, 16, 8))
-                                       for m in range(16)])
-        act("c" + T_, A("cd", no, no + C), A(b, 0, C), ACT.Copy, 0.0, 1.0 / 128)
-        act("d" + T_, A("cd", 3 * C + no, 4 * C + no), A(b, C, 2 * C), ACT.Copy, 0.0, 1.0 / 32768)
-        cut(cfg["chunks"])
-        for j, (a, b) in enumerate(ch):
-            J = T_ + "_%d" % j
-            nj = A("n16", no + a // 16, no + b // 16)
-            q, p = A("q1", a, b), A("pp", po + a, po + b)
-            s1, r = A("s1r", so + a, so + b), A("s1r", so + R + a, so + R + b)
-            gather("gq" + J, cfg["gq"][t][j], q, X(QR, nj))
-            gather("gp" + J, cfg["gp"][t][j], p, X(whole("ptab"), nj))
-            d = A(temp(), 0, b - a)
-            mm("d1a_" + J, d, [(NSEL, A("uds", 2 * t * R + a, 2 * t * R + b, 1, 8))], True, False)
-            mm("d1_" + J, d, [(TRI, q)], False, True)
-            act("s1_" + J, s1, d, ACT.Sign, 0.5, -1.0)
-            hot = []
-            pick("selq" + J, cfg["selq"][t][j], A("sel1", *pair(cfg["ga"], 0, j)), q, s1, hot)
-            pick("selp" + J, cfg["selp"][t][j], A("sel1", *pair(cfg["ga"], 1, j)), p, s1, hot)
-            d = A(temp(), 0, b - a)
-            mm("dr_" + J, d, [(WH, p), (whole("nwh"), q)])
-            act("r_" + J, r, d, ACT.Relu, 0.0, 2.0)
+            send("nh", A("nin", 3 * C, 4 * C), [A("n16", no, no + C)], 2)
+        for k, (bias, scale) in enumerate([(0.0, 2.0 ** -7), (0.0, 2.0 ** -15), (0.0, 2.0)]):
+            z, _m = turned("cd%d" % k + T_, chs, 8, [("uas", 0, 72, A("selt", 24 * t + 8 * k, 24 * t + 8 * k + 8, 1, 72))])
+            act("cde"[k] + T_, A("cd", 3 * k * C + no, 3 * k * C + no + C), z, ACT.Identity, bias, scale)
+        for ch in chs:
+            J = "1_%d_%d" % (t, ch[2])
+            either("gq" + J, "VS"[ch[2] & 1], wide("q1", ch, po), X(QR, small("n16", ch, no)), -1.0)
+            either("gp" + J, "S", wide("pp", ch, po), X(whole("ptab"), small("n16", ch, no)))
+            L, acc = draft(J, "q1", "pp", "i20", po, 2 * t, ch, "st1", "sc1"), pair("msg", ch, mo, 0)
+            test(J, L, "1", small("cd", ch, no), acc, pair("msg", ch, mo, 1), ch)
+            offsets("off" + J, "off1", to_rows("row" + J, ch, [], [(acc, IDN)]), "ra", ch, t)
+        for ch in cut(cfg["dsend"]):
+            send("d%d_%d" % (t, ch[2]), wide("din", ch, po), [wide("pp", ch, po), wide("q1", ch, po)], 1, 1)
         if t < TK - 1:
-            send("p" + T_, A("pin", po, po + R), A("pp", po, po + R), 1)
-        for k, grp in enumerate(cfg["gr"]):
-            a, b = span(grp)
-            send("r%d_%d" % (t, k), A("rin", po + a, po + b), A("s1r", so + R + a, so + R + b), 1)
-        for k, grp in enumerate(cfg["ga"]):
-            J = T_ + "_%d" % k
-            a, b = span(grp)
-            ca, cb = a // 16, b // 16
-            n, bk = cb - ca, temp()
-            mm("red1_" + J, A(bk, 0, 2 * n), to_list("sel1", 2 * a, 2 * b))
-            acc = A("msg", mo + ca, mo + cb)
-            tt("a1_" + J, A("t1", ca, cb), A(bk, 0, n), A("cd", no + ca, no + cb), ALU.mult)
-            tt("a2_" + J, acc, A(bk, n, 2 * n), A("t1", ca, cb), ALU.is_gt)
-            if cfg["zpe"] & 1:
-                z = A(temp(), 0, n)
-                mm("a3_" + J, z, [(whole("whf"), A("s2k", no + ca, no + cb)), (WH, acc)])
-                ts("a4_" + J, A("off1", ca, cb), z, 2.0 * W, None, ALU.mult)
-            else:
-                tt("a3_" + J, A("z1", ca, cb), acc, A("s2k", no + ca, no + cb), ALU.add)
-                ts("a4_" + J, A("off1", ca, cb), A("z1", ca, cb), float(W), None, ALU.mult)
-        bk = temp()
-        mm("red1b" + T_, A(bk, 0, 2 * C), to_list("s1r", so, so + 2 * R))
-        act("msg" + T_, A("msg", mo + C, mo + 3 * C), A(bk, 0, 2 * C), ACT.Copy)
-        send("m" + T_, A("mi", mo, mo + 3 * C), A("msg", mo, mo + 3 * C), 1)
-        sc1 = [cp("sc1_%d_%d" % (t, k), X(QW, A("off1", a // 16, b // 16)), A("pp", po + a, po + b))
-               for k, (a, b) in enumerate(pieces(cfg["ga"]))]
-        cut(cfg["chb"])
-        if t == 1:
-            for j, (a, b) in enumerate(ch):
-                act("h1_%d" % j, A("hh", a, b), X(whole("vtab"), A("nin", 3 * C + a // 16, 3 * C + b // 16)), ACT.Tanh)
+            send("p" + T_, A("pin", po, po + R), [A("pp", po, po + R)], 1)
+        send("m" + T_, A("mi", mo, mo + 2 * C), [A("msg", mo, mo + 2 * C)], 1)
+        for ch in chs:
+            cp("X1_%d_%d" % (t, ch[2]), X(QW, small("off1", ch)), wide("pp", ch, po))
+        for ch in thirds:
+            either("r_%d_%d" % (t, ch[2]), "S", wide("rin", ch), wide("din", ch, po), 1.0, True)
+            either("ge%d_%d" % (t, ch[2]), "S", wide("ecol", ch), X(whole("etab"), small("nin", ch, no)))
+            if t == 1:
+                prev = [add("h1_%d" % ch[2], "S", "act", (wide("hh", ch), X(whole("vtab"), small("nin", ch, 3 * C)),
+                                                          ACT.Tanh, 0.0, 1.0), [wide("hh", ch)],
+                            [X(whole("vtab"), small("nin", ch, 3 * C))], prev if ch[2] else ())]
+            if t == 2:
+                either("v2_%d" % ch[2], "S", wide("v2", ch), X(whole("vtab"), small("nin", ch, no)))
         if t == 2:
-            for j, (a, b) in enumerate(ch):
-                vj = X(whole("vtab"), A("nin", no + a // 16, no + b // 16))
-                if cfg["h2"] == "dma":
-                    act("v2_%d" % j, A("v2", a, b), vj, ACT.Copy)
-                else:
-                    tt("v2_%d" % j, A("hs", a, b), vj, A("hh", a, b), ALU.add)
-            if cfg["h2"] == "dma":
-                dma("hadd", "G", whole("hh"), whole("v2"), "hadd", 128 * R * 4, True)
-            for j, (a, b) in enumerate(ch):
-                act("h2_%d" % j, A("hh", a, b), A("hh" if cfg["h2"] == "dma" else "hs", a, b), ACT.Tanh)
-        macc, ms1, mS = A("mi", mo, mo + C), A("mi", mo + C, mo + 2 * C), A("mi", mo + 2 * C, mo + 3 * C)
-        tt("ds" + T_, whole("ds"), mS, A("cd", 3 * C + no, 4 * C + no), ALU.mult)
-        act("ab" + T_, whole("ab"), macc, ACT.Copy, 0.0, 256.0)
+            dma("hadd", "G", whole("hh"), whole("v2"), "hadd", 128 * R * 4, True)
+            for ch in thirds:
+                act("h2_%d" % ch[2], wide("hh", ch), wide("hh", ch), ACT.Tanh)
+        act("ab" + T_, whole("ab"), A("mi", mo, mo + 2 * C, 2), ACT.Copy, 0.0, 256.0)
+        z, _m = turned("S" + T_, chs, 8, [("rin", 0, 128, B8)])
+        tt("ds" + T_, whole("ds"), z, A("cd", 3 * C + no, 4 * C + no), ALU.mult)
         tt("xx" + T_, whole("xx"), whole("ds"), whole("ab"), ALU.max)
-        if t < TK - 1 and not cfg["zpe"] & 2:
-            tt("zs" + T_, whole("zs"), macc, A("s2k", no, no + C), ALU.add)
-        act("rej" + T_, whole("rej"), macc, ACT.Identity, 1.0, -1.0)
-        tt("aa" + T_, whole("aa"), macc, ms1, ALU.mult)
-        for j, (a, b) in enumerate(ch):
-            J = T_ + "_%d" % j
-            nj = A("nin", no + a // 16, no + b // 16)
-            q, r, n = A("q2", a, b), A("rin", po + a, po + b), b - a
-            s2, s3 = A("s23", *pair(cfg["gb"], 0, j)), A("s23", *pair(cfg["gb"], 1, j))
-            gather("ge" + J, cfg["ge"][t][j], A("ecol", a, b), X(whole("etab"), nj))
-            g2 = gather("gq2" + J, cfg["gq2"][t][j], q, X(QR, nj))
-            if j == 0:
-                mark = [g2]
-            d = A(temp(), 0, n)
-            mm("d2a_" + J, d, [(NSEL, A("uds", (2 * t + 1) * R + a, (2 * t + 1) * R + b, 1, 8))], True, False)
-            mm("d2_" + J, d, [(TRI, q)], False, True)
-            act("s2_" + J, s2, d, ACT.Sign, 0.5, -1.0)
-            hot = []
-            pick("selq2" + J, cfg["selq2"][t][j], A("sel2", *pair(cfg["gb"], 0, j)), q, s2, hot)
-            pick("selr" + J, cfg["selr"][t][j], A("sel2", *pair(cfg["gb"], 1, j)), r, s2, hot)
-            d = A(temp(), 0, n)
-            mm("sb_" + J, d, [(whole("blkn"), r)])
-            how, sq, w = cfg["acc"][t][j], A("sq", a, b), A("ww", a, b)
-            if how == "V":
-                tt("sq_" + J, d, d, q, ALU.mult)
-                tt("dl_" + J, d, d, r, ALU.add)
-                act("w_" + J, w, d, ACT.Relu)
-            elif how == "P":
-                tt("sq_" + J, sq, d, q, ALU.mult)
-                d = A(temp(), 0, n)
-                mm("dl_" + J, d, [(WH, r), (whole("whf"), sq)])
-                act("w_" + J, w, d, ACT.Relu, 0.0, 2.0)
+        for ch in chs:
+            J, n = "2_%d_%d" % (t, ch[2]), ch[1] - ch[0]
+            q, r, w = wide("q2", ch), wide("rin", ch), wide("ww", ch)
+            g2 = either("gq" + J, "SV"[ch[2] & 1], q, X(QR, small("nin", ch, no)), -1.0)
+            L = draft(J, "q2", "rin", "i20", 0, 2 * t + 1, ch, "st2", "sc2")
+            z = A(temp(), 0, n)
+            mm("sb" + J, [(z, [(whole("blkn"), r)])], soft=[g2])
+            tt("sq" + J, z, z, q, ALU.mult)
+            tt("z" + J, z, z, r, ALU.subtract)
+            act("w" + J, w, z, ACT.Relu, 0.0, -1.0)
+            acc, b2, p2 = pair("mi", ch, mo, 0), pair("bp", ch, 0, 0), pair("bp", ch, 0, 1)
+            test(J, L, "2", small("xx", ch), b2, p2, ch)
+            if t < TK - 1:
+                offsets("off" + J, "off2", to_rows("row" + J, ch, [], [(acc, IDN), (b2, IDN)]), "rb", ch, t)
+            z, _m = turned("c15" + J, [ch], 8, [("ww", 0, 128, whole("b8f"))])
+            nb, th, hi = n // 128, small("th", ch), pair("hl", ch, 0, 0)
+            rows = A("rt", 128 * ch[2], 128 * ch[2] + 128, 1, 16 * nb)
+            tt("ec" + J, small("ec", ch), z, small("cd", ch, 6 * C + no), ALU.mult)
+            ts("th" + J, th, small("ec", ch), 127.0 / 256, None, ALU.subtract)
+            either("hi" + J, "V", hi, small("ec", ch))
+            tt("lo" + J, pair("hl", ch, 0, 1), th, hi, ALU.subtract)
+            z = summed("tr" + J, A(temp(), 0, 128, 1, 16 * nb),
+                       [(pair("mi", ch, mo), whole("nbig")), (pair("bp", ch), whole("nbig"))], [(pair("hl", ch), IDN)])
+            act("rt" + J, rows, z, ACT.Copy, 0.0, 1.0 / 256)
+            z = A(temp(), 0, n)
+            mm("cu" + J, [(z, [(whole("ntrif"), w)])], True, False)
+            add("cv" + J, "P", "mm", [(A(z[1], b, n, nb), A("selb", 128 * b, 128 * b + 128, 1, 16 * nb), rows, False,
+                                       b == nb - 1) for b in range(nb)], [z], [whole("selb"), rows])
+            act("s3" + J, wide("s3", ch), z, ACT.Sign, 1.0 / 512)
+            J = "3_%d_%d" % (t, ch[2])
+            terms = [(pair("mi", ch, mo, 1), IDN), (acc, whole("n143")), (p2, IDN), (b2, whole("n143"))]
+            third = [(A("hb", 24 - 8 * b, 24 - 8 * b + 8 * nb), x) for b, x in enumerate(blocks("s3", ch))]
+            act("v" + J, rows_of("rv", ch), to_rows("row" + J, ch, terms, third), ACT.Identity, 15.0, -1.0)
+            kj, e = small("k16", ch), wide("ecol", ch)
+            cp("k16" + J, kj, to_list("k" + J, ch, [], from_rows("rk", "rv", ch)))
+            if cfg["sele"][t][ch[2]] == "V":
+                tt("sele" + J, wide("sele", ch), X(whole("idv"), kj), e, ALU.mult)
             else:
-                tt("sq_" + J, sq, d, q, ALU.mult)
-                dma("dl_" + J, "G", sq, r, "dl_" + J, 128 * n * 8, True)
-                act("w_" + J, w, sq, ACT.Relu)
-            d = A(temp(), 0, n)
-            mm("eb_" + J, d, [(NSEL, A("uas", (3 * t + 2) * R + a, (3 * t + 2) * R + b, 1, 8))])
-            tt("ew_" + J, A("ew", a, b), d, w, ALU.mult)
-            d = A(temp(), 0, n)
-            mm("cu_" + J, d, [(whole("trif"), w)], True, False)
-            mm("cv_" + J, d, [(whole("blkf"), A("ew", a, b))], False, True)
-            act("s3_" + J, s3, d, ACT.Sign, 1.0 / 512, -1.0)
-        for k, grp in enumerate(cfg["gb"]):
-            J = T_ + "_%d" % k
-            a, b = span(grp)
-            ca, cb = a // 16, b // 16
-            n, bk = cb - ca, temp()
-            b2, b3 = A("beta", 2 * ca, 2 * ca + n), A("beta", 2 * ca + n, 2 * cb)
-            mm("red2_" + J, A(bk, 0, 2 * n), to_list("sel2", 2 * a, 2 * b))
-            tt("b1_" + J, A("t2", ca, cb), A(bk, 0, n), A("xx", ca, cb), ALU.mult)
-            tt("b2_" + J, b2, A(bk, n, 2 * n), A("t2", ca, cb), ALU.is_gt)
-            tt("b5_" + J, b3, A("rej", ca, cb), b2, ALU.subtract)
-            if t < TK - 1 and cfg["zpe"] & 2:
+                act("hot" + J, wide("hot", ch), X(whole("ids"), kj), ACT.Copy)
                 z = A(temp(), 0, n)
-                mm("b3_" + J, z, [(whole("whf"), A("s2k", no + ca, no + cb)), (WH, A("mi", mo + ca, mo + cb)), (WH, b2)])
-                ts("b4_" + J, A("off2", ca, cb), z, 2.0 * W, None, ALU.mult)
-            elif t < TK - 1:
-                tt("b3_" + J, A("z2", ca, cb), b2, A("zs", ca, cb), ALU.add)
-                ts("b4_" + J, A("off2", ca, cb), A("z2", ca, cb), float(W), None, ALU.mult)
-            bk = temp()
-            mm("red3_" + J, A(bk, 0, 2 * n), to_list("s23", 2 * a, 2 * b))
-            tt("c1_" + J, A("prod", 2 * ca, 2 * cb), A(bk, 0, 2 * n), A("beta", 2 * ca, 2 * cb), ALU.mult)
-            three = [A("aa", ca, cb), A("prod", 2 * ca, 2 * ca + n), A("prod", 2 * ca + n, 2 * cb)]
-            bk = temp()
-            mm("kk_" + J, A(bk, 0, n), [(whole("sh"), x) for x in three])
-            ts("c2_" + J, A("k16", ca, cb), A(bk, 0, n), A("kc", 0, 1), None, ALU.add)
-            for j in grp:
-                a1, b1 = ch[j]
-                J1 = T_ + "_%d" % j
-                kj, e = A("k16", a1 // 16, b1 // 16), A("ecol", a1, b1)
-                if cfg["sele"][t][j] == "V":
-                    tt("sele" + J1, A("sele", a1, b1), X(whole("idv"), kj), e, ALU.mult)
-                else:
-                    act("hot" + J1, A("hot", a1, b1), X(whole("ids"), kj), ACT.Copy)
-                    d = A(temp(), 0, b1 - a1)
-                    mm("de_" + J1, d, [(WH, e), (WH, A("hot", a1, b1))])
-                    act("sele" + J1, A("sele", a1, b1), d, ACT.Relu, -2048.0, 32.0)
-            bk = temp()
-            mm("nn_" + J, A(bk, 0, n), [(WH, x) for x in three] + to_list("sele", a, b))
-            ts("c3_" + J, A("n16", no + C + ca, no + C + cb), A(bk, 0, n), 8.0, None, ALU.add)
-            act("nf" + J, A("nf", no + ca, no + cb), A(bk, 0, n), ACT.Identity, 8.0)
+                mm("de" + J, [(z, [(IDN, e), (IDN, wide("hot", ch))])])
+                act("sele" + J, wide("sele", ch), z, ACT.Relu, -2048.0, 16.0)
+            z = to_list("nn" + J, ch, from_rows("rl", "rv", ch),
+                        [(A("zz", 15 - m, 143 - m), A("sele", ch[0] + m, ch[1], 16)) for m in range(16)])
+            cp("n" + J, small("n16", ch, no + C), z)
+            act("nf" + J, small("nf", ch, no), z, ACT.Copy)
         if t < TK - 1:
-            for k, (a, b) in enumerate(pieces(cfg["gb"])):
-                cp("sc2_%d_%d" % (t, k), X(QW, A("off2", a // 16, b // 16)), A("pin", po + a, po + b))
+            for ch in chs:
+                cp("X2_%d_%d" % (t, ch[2]), X(QW, small("off2", ch)), wide("pin", ch, po))
     dma("st_n", "Y", D("yn"), whole("nf"), "st", 128 * C * 12)
-    for j, (a, b) in enumerate(ch):
-        tt("v3_%d" % j, A("hs", a, b), X(whole("vtab"), A("n16", 3 * C + a // 16, 3 * C + b // 16)), A("hh", a, b), ALU.add)
-        act("h3_%d" % j, A("ho", a, b), A("hs", a, b), ACT.Tanh)
-        dma("st_h%d" % j, "Y", D("yh", a, b), A("ho", a, b), "st", 128 * (b - a) * 4)
+    for ch in cut(cfg.get("tail", cfg["chunks"][2])):
+        tt("v3_%d" % ch[2], wide("hs", ch), X(whole("vtab"), small("n16", ch, 3 * C)), wide("hh", ch), ALU.add)
+        act("h3_%d" % ch[2], wide("ho", ch), wide("hs", ch), ACT.Tanh)
+        dma("st_h%d" % ch[2], "Y", D("yh", ch[0], ch[1]), wide("ho", ch), "st", 128 * (ch[1] - ch[0]) * 4)
     return ops
 
 
-def plan(cfg, m=None):
-    ops = graph(cfg)
-    order, bank_of, end, holder, users = cfg.get("order", list(range(len(ops)))), {}, 0.0, {}, {}
-    if isinstance(order, str):
-        order = [DIGITS.index(order[k]) * 32 + DIGITS.index(order[k + 1]) for k in range(0, len(order), 2)]
+COST = {"cycle": 0.83, "pe": 0.42, "gather": 1.5, "scatter": 3.2, "hop": 160.0, "dma": 1800.0, "hbm": 250.0,
+        "send": 2000.0, "link": 70.0, "issue": 400.0, "first": 1500.0}
+SPREAD = [{}, {"cycle": 1.2, "pe": 0.6, "gather": 1.9, "scatter": 5.0},
+          {"gather": 1.2, "scatter": 2.2, "hop": 260.0, "link": 50.0, "send": 3000.0, "issue": 800.0}]
+HEAT, REACH, PULL, STRIDE = 0.0006, 40, 0.5, 48
+
+
+def cost_of(o, k):
+    c, a = o["call"], o["args"]
+
+    def narrow(x):
+        return x[1][0] != "@" and SIZE[SB[x[1]][0]] == 2
+
+    if c == "mm":
+        return k["pe"] * sum(max(min(64, count_of(x)), count_of(y)) * (1 if narrow(x) else 4) for _o, x, y, _s, _e in a)
+    if c in ("dma", "send"):
+        return (k["issue"] if o["eng"] == "G" else 60.0) + (k["first"] if o["name"] in ("n0", "hadd") else 0.0)
+    n = count_of(a[0])
+    if o["name"] == "h1_0":
+        n += 1300.0 / k["cycle"] / k["gather"]
+    if c in ("sel", "iota"):
+        return 170.0 + 2 * n * k["cycle"]
+    aps = [x for x in a if isinstance(x, tuple)]
+    if a[0][0] == "ind":
+        return 50.0 + k["scatter"] * n * k["cycle"]
+    if any(x[0] == "ind" for x in aps):
+        return 60.0 + k["gather"] * n * k["cycle"]
+    if c == "tt":
+        n *= 1 if a[1][1][0] == "@" or a[2][1][0] == "@" else 2
+    elif o["eng"] == "V" and all(narrow(x) for x in aps):
+        n *= 0.5
+    return max(64, n) * k["cycle"]
+
+
+def schedule(ops, k, slack):
+    n = len(ops)
+    cost = [cost_of(o, k) for o in ops]
+    lag = [k["hop"] if o["kind"] == "c" else
+           (k["dma"] + o["nbytes"] / k["hbm"] if o["kind"] == "dma" else k["send"] + o["nbytes"] / k["link"]) for o in ops]
+    after = [[] for _o in ops]
+    for o in ops:
+        for d in o["deps"] | o["soft"]:
+            after[d].append(o["i"])
+    way = [0.0] * n
+    for i in reversed(range(n)):
+        way[i] = cost[i] + lag[i] + max([way[j] for j in after[i]], default=0.0)
+    users = {}
     for o in ops:
         for tp in o["temps"]:
             users.setdefault(tp, []).append(o["i"])
-    for i in order:
-        for tp in ops[i]["temps"]:
+    left = [len(o["deps"] | o["soft"]) for o in ops]
+    ready = [i for i in range(n) if not left[i]]
+    done, began, free = {}, {}, {}
+    bank_of, holder, order = {}, {}, []
+    while ready:
+        open_banks = sorted((max([done[u] for u in users.get(holder.get(b), [])], default=0.0), b) for b in range(8)
+                            if all(u in done for u in users.get(holder.get(b), [])))
+        cand = []
+        for i in ready:
+            o = ops[i]
+            s = max([free.get(o["eng"], 0.0)] + [done[d] for d in o["deps"]] + [began[d] for d in o["soft"]])
+            if any(tp not in bank_of for tp in o["temps"]):
+                if not open_banks:
+                    continue
+                s = max(s, open_banks[0][0])
+            cand.append((s, i))
+        first = min(cand)
+        s, i = max((c for c in cand if c[0] <= first[0] + slack and ops[c[1]]["eng"] == ops[first[1]]["eng"]),
+                   key=lambda c: way[c[1]])
+        o = ops[i]
+        for tp in o["temps"]:
             if tp not in bank_of:
-                bk = int(cfg["banks"][len(bank_of)]) if "banks" in cfg else len(bank_of) % 8
-                bank_of[tp] = bk
-                ops[i]["deps"] = ops[i]["deps"] | set(users.get(holder.get(bk), []))
-                holder[bk] = tp
+                b = open_banks[0][1]
+                bank_of[tp], holder[b] = b, tp
+        began[i], free[o["eng"]] = s, s + cost[i]
+        done[i] = s + cost[i] + lag[i]
+        order.append(i)
+        ready.remove(i)
+        for j in after[i]:
+            left[j] -= 1
+            if not left[j]:
+                ready.append(j)
+    return order
+
+
+def refine(ops, order, steps, seed):
+    n = len(ops)
+    engines = "VSPGY"
+    above = [0] * n
+    need = []
+    for o in ops:
+        keep, seen = [], 0
+        for d in sorted(o["deps"] | o["soft"], reverse=True):
+            if not seen >> d & 1:
+                keep.append(d)
+            seen |= above[d] | 1 << d
+        above[o["i"]] = seen
+        need.append(keep)
+    after = [[] for _o in ops]
+    for i in range(n):
+        for d in need[i]:
+            after[d].append(i)
+    users = {}
+    for o in ops:
+        for tp in o["temps"]:
+            users.setdefault(tp, []).append(o["i"])
+    opens = [[tp for tp in o["temps"] if users[tp][0] == o["i"]] for o in ops]
+    eng = [engines.index(o["eng"]) for o in ops]
+    either = [o["i"] for o in ops if o["call"] == "either"]
+    sets = [dict(COST, **d) for d in SPREAD]
+    cost = [[[cost_of(dict(o, eng=e), k) for e in "VS"] if o["call"] == "either" else [cost_of(o, k)] * 5 for o in ops]
+            for k in sets]
+    kind = [["c", "dma", "send"].index(o["kind"]) for o in ops]
+    weak = [[d for d in need[i] if d in ops[i]["deps"] and d not in ops[i]["reads"] and not kind[i] and not kind[d]]
+            for i in range(n)]
+    firm = [[d for d in need[i] if d in ops[i]["deps"] and d not in weak[i]] for i in range(n)]
+
+    def run(order, m, extra, marks, since):
+        k, cm = sets[m], cost[m]
+        hop, fixed, rate = k["hop"], [0.0, k["dma"], k["send"]], [1.0, k["hbm"], k["link"]]
+        free, pipe, done, holder = [list(x) for x in marks[since]]
+        first = m == 0
+        del marks[since + 1:]
+        for at in range(since * STRIDE, n):
+            if at % STRIDE == 0 and at > since * STRIDE:
+                marks.append((list(free), list(pipe), list(done), list(holder)))
+            i = order[at]
+            e = eng[i]
+            s = free[e]
+            for d in firm[i]:
+                if done[d] > s:
+                    s = done[d]
+            for d in weak[i]:
+                if eng[d] != e and done[d] > s:
+                    s = done[d]
+            if opens[i]:
+                if first:
+                    best = None
+                    for b in range(8):
+                        since_b = 0.0
+                        for u in holder[b]:
+                            if done[u] is None:
+                                since_b = None
+                                break
+                            if done[u] > since_b:
+                                since_b = done[u]
+                        if since_b is not None and (best is None or since_b < best[0]):
+                            best = (since_b, b)
+                    if best is None:
+                        return None
+                    extra[i] = (best[1], holder[best[1]])
+                    holder[best[1]] = users[opens[i][0]]
+                for u in extra[i][1]:
+                    if done[u] > s:
+                        s = done[u]
+            s += cm[i][e]
+            free[e] = s
+            if kind[i]:
+                s = max(s + fixed[kind[i]], pipe[kind[i]]) + ops[i]["nbytes"] / rate[kind[i]]
+                pipe[kind[i]] = s
+                done[i] = s
+            else:
+                done[i] = s + hop
+        return max(done) + PULL * sum(done) / n
+
+    def value(order, extra, marks, since):
+        extra, marks, total = dict(extra), [list(x) for x in marks], 0.0
+        for m in range(len(sets)):
+            t = run(order, m, extra, marks[m], since)
+            if t is None:
+                return None, extra, marks
+            total += t / base[m]
+        return total, extra, marks
+
+    extra, marks = {}, [[([0.0] * 5, [0.0] * 3, [None] * n, [()] * 8)] for _k in sets]
+    base = [run(order, m, extra, marks[m], 0) for m in range(len(sets))]
+    now = float(len(sets))
+    best = (now, list(order), list(eng), extra)
+    rng = np.random.default_rng(seed)
+    for step, (a, b, c, u) in enumerate(rng.random((steps, 4)).tolist()):
+        if a < 0.04:
+            i = either[int(b * len(either))]
+            eng[i] = 1 - eng[i]
+            new, low = order, order.index(i)
+        else:
+            at = int(b * n)
+            i = order[at]
+            lo = max([order.index(d) for d in need[i]], default=-1) + 1
+            hi = min([order.index(d) for d in after[i]], default=n) - 1
+            near = [p for p in range(max(lo, at - REACH), min(hi, at + REACH) + 1) if p != at and eng[order[p]] == eng[i]]
+            if not near:
+                continue
+            new = order[:at] + order[at + 1:]
+            new.insert(near[int(c * len(near))], i)
+            low = min(at, near[int(c * len(near))])
+        v, ex, mk = value(new, extra, marks, low // STRIDE)
+        if v is not None and v <= now - HEAT * (1.0 - step / steps) * math.log(1.0 - u):
+            now, order, extra, marks = v, new, ex, mk
+            if v < best[0]:
+                best = (v, list(order), list(eng), ex)
+        elif a < 0.04:
+            eng[i] = 1 - eng[i]
+    bank_of = {}
+    for o in ops:
+        o["eng"] = engines[best[2][o["i"]]]
+    for i, (b, before) in best[3].items():
+        bank_of[opens[i][0]] = b
+        ops[i]["deps"] = ops[i]["deps"] | set(before)
+    return best[1], bank_of
+
+
+def plan(cfg):
+    ops = graph(cfg)
+    order, bank_of = refine(ops, schedule(ops, COST, cfg["slack"]), cfg["steps"], cfg["seed"])
     pos, know, clock, need, cnt = {}, {}, {}, set(), {}
     for i in order:
         o = ops[i]
@@ -399,15 +593,13 @@ def plan(cfg, m=None):
         o["waits"] = []
         for d in sorted(o["deps"], key=lambda x: -pos[x][2]):
             line, at = pos[d][0], pos[d][1]
-            if k.get(line, -1) >= at:
+            if k.get(line, -1) >= at or (d not in o["reads"] and line == e and o["kind"] == "c"):
                 continue
             o["waits"].append(d)
             need.add(d)
             for l2, a2 in clock[d].items():
                 k[l2] = max(k.get(l2, -1), a2)
         line = e if o["kind"] == "c" else o["sem"]
-        if o["kind"] == "dma":
-            o["val"] = 16 * sum(1 for x in ops if x.get("sem") == o["sem"])
         cnt[line] = cnt.get(line, -1) + 1
         pos[i] = (line, cnt[line], len(pos))
         clock[i] = {} if o["kind"] == "send" else dict(k)
@@ -419,7 +611,7 @@ def plan(cfg, m=None):
         if o["kind"] == "c" and o["inc"]:
             total[o["eng"]] = total.get(o["eng"], 0) + 1
             o["val"] = total[o["eng"]]
-    return {"ops": ops, "order": order, "bank": bank_of, "end": end, "total": total}
+    return {"ops": ops, "order": order, "bank": bank_of, "total": total}
 
 
 PLAN = plan(CFG)
@@ -441,8 +633,6 @@ def rank_program(g, core, T, topo):
         if x[0] == "dram":
             return T[x[1]][:] if x[2] is None else T[x[1]][:, x[2]:x[3]]
         name = "bank%d" % PLAN["bank"][x[1]] if x[1][0] == "@" else x[1]
-        if isinstance(x[5], tuple):
-            return T[name][x[5][0]:x[5][1]:x[5][2], x[2]:x[3]]
         if x[4] == 1:
             return T[name][0:x[5], x[2]:x[3]]
         return T[name][0:x[5], x[2]:x[3]:x[4]]
@@ -459,11 +649,16 @@ def rank_program(g, core, T, topo):
             if od["kind"] == "c":
                 q.wait_ge(T.sem["e" + od["eng"]], od["val"])
             else:
-                q.wait_ge(T.sem[od["sem"]], od["val"] if od["kind"] == "dma" else arrivals(od["args"][2]))
+                q.wait_ge(T.sem[od["sem"]], 16 if od["kind"] == "dma" else arrivals(od["args"][2]))
         if c == "send":
             dst = T.cores[(rank + a[2]) % N]
             rid, pid, _se = topo.addr(dst)
-            g.remote_dma(ap(a[0]), ap(a[1]), T.sem[o["sem"]], T.sem["sent"], pid, rid, topo.mask(core, dst))
+            if a[3]:
+                g.remote_dma_fused([RemoteDMATransfer(
+                    dst_ids=[DstId(rid=rid, pnc=pid)], dma_engine_mask=topo.mask(core, dst), remote_sem=T.sem[o["sem"]],
+                    srcs=[ap(x) for x in a[1]], dsts=[ap(a[0])], alu_op=a[3])], local_sem=T.sem["sent"])
+            else:
+                g.remote_dma(ap(a[0]), ap(a[1][0]), T.sem[o["sem"]], T.sem["sent"], pid, rid, topo.mask(core, dst))
             sent[0] += len(topo.engines(core, dst))
             continue
         if c == "dma":
@@ -472,8 +667,8 @@ def rank_program(g, core, T, topo):
             stores[0] += 16 if o["sem"] == "st" else 0
             continue
         if c == "mm":
-            for k, (x, y) in enumerate(a[1]):
-                ins = q.matmul(ap(a[0]), ap(x), ap(y), a[2] and k == 0, a[3] and k == len(a[1]) - 1)
+            for out, x, y, start, stop in a:
+                ins = q.matmul(ap(out), ap(x), ap(y), start, stop)
         elif c == "tt":
             ins = q.tensor_tensor(ap(a[0]), ap(a[1]), ap(a[2]), a[3])
         elif c == "ts":
@@ -483,14 +678,22 @@ def rank_program(g, core, T, topo):
                 ins = q.tensor_scalar(ap(a[0]), ap(a[1]), ap(a[2]), ap(a[3]), a[4], a[5])
         elif c == "cp":
             ins = q.tensor_copy(ap(a[0]), ap(a[1]))
+        elif c == "scan":
+            ins = q.tensor_tensor_scan(ap(a[0]), ap(a[1]), ap(a[2]), 0.0, ALU.mult, ALU.max)
         elif c == "act":
             ins = q.activation(ap(a[0]), ap(a[1]), a[2], bias=a[3], scale=a[4])
+        elif c == "either" and o["eng"] == "S":
+            ins = q.activation(ap(a[0]), ap(a[1]), ACT.Relu if a[3] else ACT.Copy, bias=0.0, scale=a[2])
+        elif c == "either":
+            ins = q.tensor_scalar(ap(a[0]), ap(a[1]), 0.0 if a[3] else a[2], None, ALU.max if a[3] else ALU.mult)
         elif c == "fill":
             ins = q.memset(ap(a[0]), a[1])
         elif c == "sel":
             ins = q.affine_select(ap(a[0]), ap(a[1]), a[2], a[3], 0.0, a[4], a[5])
-        else:
+        elif SB[a[0][1]][0] == I32:
             ins = q.iota(ap(a[0]), a[1], a[2], a[3])
+        else:
+            ins = q.iota(ap(a[0]), a[1], a[2], a[3], allow_small_or_imprecise_dtypes=True)
         if o["inc"]:
             ins.then_inc(T.sem["e" + o["eng"]], 1)
     for e, v in PLAN["total"].items():

import math
import numpy as np
from concourse.bass import DstId, RemoteDMATransfer
from concourse.mybir import AluOpType, ActivationFunctionType

ALU = AluOpType
ACT = ActivationFunctionType
R, W, TK, C = 1536, 2048, 3, 96

CFG = {
    "chunks": [[512, 512, 512]] * 3, "sele": ["SVV", "SVV", "VVV"], "dsend": [512, 512, 512],
    "split": ["row", "nn"], "early": ["---", "bb-", "---", "bb-", "---", "bb-"],
    "loads": "nq0psadev", "slack": 60.0, "steps": 130000, "seed": 1,
}

BF, F32, I32, U16 = "bfloat16", "float32", "int32", "uint16"
SB = {
    "qw": (BF, 2 * W), "ptab": (BF, W), "etab": (BF, W), "vtab": (BF, W), "uds": (BF, R), "uas": (BF, R),
    "n0s": (I32, C), "sps": (I32, 3 * C), "sph": (BF, 3 * C), "spl": (BF, 3 * C), "cd": (F32, 9 * C),
    "ec": (F32, C), "th": (I32, C), "hl": (BF, 2 * C), "rt": (BF, 768), "selb0": (BF, 512), "selb": (BF, 512),
    "n16": (U16, 4 * C), "nin": (U16, 4 * C), "off1": (U16, C), "off2": (U16, C), "k16": (U16, C),
    "q1": (BF, 3 * R), "pp": (BF, 3 * R), "din": (BF, 3 * R), "pin": (BF, 2 * R), "rin": (BF, R),
    "q2": (BF, R), "ecol": (BF, R), "hot": (BF, R), "sele": (BF, R), "v2": (BF, R), "s3": (BF, R),
    "st1": (BF, R), "st2": (BF, R), "sc1": (F32, R), "sc2": (F32, R),
    "ww": (F32, R), "hh": (F32, R), "hs": (F32, R), "ho": (F32, R),
    "msg": (BF, 6 * C), "mi": (BF, 6 * C), "ds": (F32, C), "ud0": (BF, R),
    "li1": (I32, C), "qi1": (I32, C), "lo1": (I32, C), "tb1": (F32, C), "y1": (BF, C),
    "li2": (I32, C), "qi2": (I32, C), "lo2": (I32, C), "tb2": (F32, C), "y2": (BF, C),
    "ab": (F32, C), "xx": (F32, C), "bp": (BF, 2 * C),
    "nf": (F32, 3 * C), "ra": (BF, 768), "rb": (BF, 768), "rv": (BF, 768),
    "one": (BF, 640), "blk0": (BF, 144), "blk": (BF, 144), "zz": (BF, 144), "idn": (BF, 128), "tris": (BF, 128),
    "tri": (BF, 128), "ntrif": (F32, 128), "b8f": (F32, 8), "blkn": (BF, 128), "n143": (BF, 128),
    "nbig": (BF, 128), "zer": (BF, 512),
    "y4": (BF, 128), "m0": (BF, 128), "m1": (BF, 128), "pk": (BF, 128), "i20": (BF, 128),
    "h0": (BF, 8), "h1": (BF, 8), "hb": (BF, 56), "rl": (BF, 144), "rk": (BF, 144), "nsu": (BF, 768),
    "selt": (BF, 72), "id0": (I32, 32), "id1": (I32, 32), "idv": (BF, 32), "ids": (BF, 32),
}
SIZE = {BF: 2, F32: 4, I32: 4, U16: 2}
SCRATCH = {k: ("sbuf", [128, v[1]], v[0]) for k, v in SB.items()}
for _b in range(8):
    SCRATCH["bank%d" % _b] = ("psum", [128, 512], "float32")


def A(name, a, b, step=1, rows=128):
    return ("ap", name, a, b, step, rows)


def X(win, off):
    return ("ind", win, off)


def D(name, a=None, b=None):
    return ("dram", name, a, b)


def parts_of(x):
    if isinstance(x, tuple) and x[0] == "ap":
        return [x]
    if isinstance(x, tuple) and x[0] == "ind":
        return [x[1], x[2]]
    return []


def count_of(x):
    return 16 * (x[2][3] - x[2][2]) if x[0] == "ind" else len(range(x[2], x[3], x[4]))


def graph(cfg):
    ops, seen, nt = [], {}, [0]

    def temp():
        nt[0] += 1
        return "@%d" % nt[0]

    def add(name, eng, call, args, outs, ins, soft=(), **kw):
        i = len(ops)
        deps, reads, acc = set(), set(), []
        for o in outs:
            ps = parts_of(o)
            acc += [(ps[0], True)] + [(p, False) for p in ps[1:]] if ps else []
        for o in ins:
            acc += [(p, False) for p in parts_of(o)]
        for p, wr in acc:
            bank = p[1][0] == "@"
            for (a, b, j, w2) in seen.get(p[1], []):
                if (wr or w2 or ops[j]["eng"] != eng) if bank else (a < p[3] and p[2] < b and (wr or w2)):
                    deps.add(j)
                    if w2 and not (wr and eng == "P"):
                        reads.add(j)
        for p, wr in acc:
            seen.setdefault(p[1], []).append((p[2], p[3], i, wr))
        deps.discard(i)
        op = {"i": i, "name": name, "eng": eng, "call": call, "args": args, "deps": deps, "reads": reads,
              "soft": set(soft), "temps": sorted({p[1] for p, _w in acc if p[1][0] == "@"}), "kind": "c"}
        op.update(kw)
        ops.append(op)
        return i

    def mm(name, sums, start=True, stop=True, soft=()):
        calls = [(o, x, y, start and k == 0, stop and k == len(terms) - 1)
                 for o, terms in sums for k, (x, y) in enumerate(terms)]
        return add(name, "P", "mm", calls, [c[0] for c in calls], [x for c in calls for x in c[1:3]], soft)

    def tt(name, out, a, b, op):
        return add(name, "V", "tt", (out, a, b, op), [out], [a, b])

    def ts(name, out, a, s1, s2, op0, op1=None):
        return add(name, "V", "ts", (out, a, s1, s2, op0, op1), [out], [a, s1, s2])

    def cp(name, out, a):
        return add(name, "V", "cp", (out, a), [out], [a])

    def scan(name, out, a, b):
        return add(name, "V", "scan", (out, a, b), [out], [a, b])

    def act(name, out, a, func, bias=0.0, scale=1.0):
        return add(name, "S", "act", (out, a, func, bias, scale), [out], [a])

    def either(name, eng, out, a, scale=1.0, relu=False):
        return add(name, eng, "either", (out, a, scale, relu), [out], [a])

    def fill(name, out, v):
        return add(name, "V", "fill", (out, v), [out], [])

    def select(name, out, a, pat, op, base, cm):
        return add(name, "G", "sel", (out, a, pat, op, base, cm), [out], [a])

    def iota(name, out, pat, base, cm):
        return add(name, "G", "iota", (out, pat, base, cm), [out], [])

    def dma(name, eng, out, a, sem, nbytes, accum=False, soft=()):
        return add(name, eng, "dma", (out, a, accum), [out], [a] + ([out] if accum else []), soft, kind="dma", sem=sem,
                   nbytes=nbytes)

    def send(name, out, srcs, hop, alu=0):
        return add(name, "G", "send", (out, srcs, hop, alu), [out], srcs, kind="send", sem=name,
                   nbytes=128 * count_of(out) * SIZE[SB[out[1]][0]])

    def whole(n, rows=128):
        return A(n, 0, SB[n][1], 1, rows)

    def cut(sizes):
        return [(sum(sizes[:k]), sum(sizes[:k + 1]), k) for k in range(len(sizes))]

    def wide(buf, ch, at=0):
        return A(buf, at + ch[0], at + ch[1])

    def small(buf, ch, at=0):
        return A(buf, at + ch[0] // 16, at + ch[1] // 16)

    def pair(buf, ch, at=0, k=None):
        return A(buf, at + ch[0] // 8 + (k or 0), at + ch[1] // 8, 1 if k is None else 2)

    def blocks(buf, ch, at=0, rows=128):
        nb = (ch[1] - ch[0]) // 128
        return [A(buf, at + ch[0] + b, at + ch[1], nb, rows) for b in range(nb)]

    def turned(name, chs, width, terms, soft=()):
        bk, sums = temp(), []
        for ch in chs:
            for b in range((ch[1] - ch[0]) // 128):
                at = width * len(sums)
                sums.append((A(bk, at, at + width), [(blocks(x, ch, o, rows)[b], y) for x, o, rows, y in terms]))
        return A(bk, 0, width * len(sums)), mm(name, sums, soft=soft)

    def turned_early(name, ch, early, late, soft=()):
        bk, nb = temp(), (ch[1] - ch[0]) // 128
        out = A(bk, 0, 128 * nb)
        for tag, (x, o, rows, y) in (("a", early), ("", late)):
            calls = [(A(bk, 128 * b, 128 * b + 128), blocks(x, ch, o, rows)[b], y, False, not tag and b == nb - 1)
                     for b in range(nb)]
            if tag:
                calls.insert(0, (out, A("zer", 0, 128, 1, 32), A("zer", 0, 128 * nb, 1, 32), True, False))
            m = add(name + tag, "P", "mm", calls, [out], [v for c in calls for v in c[1:3]], () if tag else soft)
        return out, m

    def summed(name, out, early, late):
        if early and name.rstrip("0123456789_l") in cfg["split"]:
            mm(name + "a", [(out, early)], True, False)
            mm(name, [(out, late)], False)
        else:
            mm(name, [(out, early + late)])
        return out

    def to_rows(name, ch, early, late):
        return summed(name, A(temp(), 0, 128, 1, (ch[1] - ch[0]) // 16), early, late)

    def rows_of(buf, ch):
        return A(buf, 128 * ch[2], 128 * ch[2] + 128, 1, (ch[1] - ch[0]) // 16)

    def from_rows(mat, buf, ch):
        nb = (ch[1] - ch[0]) // 128
        return [(A(mat, 16 - nb * u, 144 - nb * u, 1, 8 * nb),
                 A(buf, 128 * ch[2] + u, 128 * ch[2] + 128, 16 // nb, 8 * nb)) for u in range(16 // nb)]

    def to_list(name, ch, early, late):
        return summed(name, A(temp(), 0, (ch[1] - ch[0]) // 16), early, late)

    def offsets(name, out, rows, buf, ch, t):
        act(name + "r", rows_of(buf, ch), rows, ACT.Copy, 0.0, float(W))
        cp(name, small(out, ch), to_list(name + "l", ch, [(IDN, small(s, ch, t * C)) for s in ("sph", "spl")],
                                         from_rows("rl", buf, ch)))

    def draft(J, q, low, ilow, at, kind, ch, st, sc):
        how = cfg["early"][kind][ch[2]]
        x, y = (q, at, 128, TRIS), ("uds", 0, 48, A("nsu", 128 * kind, 128 * kind + 128, 1, 48))
        if kind == 0:
            y = ("ud0", 0, 8, A("nsu", 0, 128, 1, 8))
        u, m = turned_early("cum" + J, ch, y, x) if how in "ub" else turned("cum" + J, [ch], 128, [x, y])
        act("st" + J, wide(st, ch), u, ACT.Sign, -0.5, -1.0)
        x, y = (q, at, 128, whole("pk")), (low, at, 128, whole(ilow))
        v, m = turned_early("pk" + J, ch, y, x, [m]) if how in "rb" else turned("pk" + J, [ch], 128, [x, y], [m])
        scan("sc" + J, wide(sc, ch), wide(st, ch), v)
        return A(sc, ch[0] + 15, ch[1], 16)

    def test(J, L, k, factor, yes, token, ch):
        li, q, low, bound, y = [small(x + k, ch) for x in ("li", "qi", "lo", "tb", "y")]
        ts("li" + J, li, L, 2.0 ** 20, None, ALU.mult)
        ts("q" + J, q, li, 10, 1023, ALU.logical_shift_right, ALU.bitwise_and)
        ts("r" + J, low, li, 1023, None, ALU.bitwise_and)
        tt("t" + J, bound, q, factor, ALU.mult)
        tt("yes" + J, yes, low, bound, ALU.is_gt)
        act("y" + J, y, L, ACT.Identity, 128.0)
        tt("tok" + J, token, y, yes, ALU.mult)

    QW, QR, IDN, TRIS = whole("qw"), A("qw", 0, W), whole("idn"), whole("tris")
    BLK, B8 = A("blk", 0, 128), A("blk", 0, 128, 16)
    thirds = cut([512, 512, 512])

    loads = {"n": (whole("n0s"), D("n0"), 128 * C * 4), "q": (QR, D("qd"), 128 * W * 2),
             "p": (whole("ptab"), D("pt"), 128 * W * 2), "d": (whole("uds", 48), D("ud"), 48 * R * 2),
             "0": (whole("ud0", 8), D("ud", 0, R), 8 * R * 2),
             "a": (whole("uas", 72), D("ua"), 72 * R * 2), "s": (whole("sps"), D("spot"), 128 * C * 12),
             "e": (whole("etab"), D("nx"), 128 * W * 2), "v": (whole("vtab"), D("vf"), 128 * W * 2)}
    prev = []
    for k in cfg["loads"]:
        prev = [dma("ld_" + k, "Y", loads[k][0], loads[k][1], "ld_" + k, loads[k][2], soft=prev)]
    fill("one", whole("one"), 1.0)
    fill("zer", whole("zer", 32), 0.0)
    select("blk0", whole("blk0"), A("one", 0, 144), [[-16, 9], [0, 16]], ALU.is_ge, 0, 1)
    select("blk", whole("blk"), whole("blk0"), [[16, 9], [0, 16]], ALU.is_ge, 15, -1)
    select("tris", TRIS, BLK, [[1, 128]], ALU.is_ge, -1, -1)
    select("nsu0", A("nsu", 0, 128, 1, 8), A("one", 0, 128, 1, 8), [[-1, 8], [0, 16]], ALU.is_equal, 0, 1)
    select("idn", IDN, A("one", 0, 128), [[-1, 128]], ALU.is_equal, 0, 1)
    iota("y4", whole("y4"), [[0, 8], [-4, 16]], 60, 0)
    select("selt", whole("selt", 72), A("one", 0, 72, 1, 72), [[-1, 9], [-9, 8]], ALU.is_equal, 0, 1)
    fill("rl0", A("rl", 0, 16, 1, 32), 0.0)
    select("rl", A("rl", 16, 144, 1, 32), A("one", 0, 128, 1, 32), [[-1, 8], [100, 4], [-8, 4]], ALU.is_equal, 0, 1)
    select("nsu1", A("nsu", 128, 768, 1, 48), whole("one", 48), [[-1, 5], [-6, 8], [0, 16]], ALU.is_equal, -1, 1)
    select("selb0", whole("selb0", 64), A("one", 0, 512, 1, 64), [[-16, 4], [-2, 8], [0, 16]], ALU.is_ge, 0, 1)
    select("selb", whole("selb", 64), whole("selb0", 64), [[16, 4], [2, 8], [0, 16]], ALU.is_ge, 1, -1)
    select("zz", whole("zz"), whole("blk"), [[0, 9], [1, 16]], ALU.is_equal, -15, 0)
    iota("id0", whole("id0"), [[-1, 32]], 32, 1)
    tt("m0", whole("m0"), whole("y4"), BLK, ALU.mult)
    tt("m1", whole("m1"), whole("m0"), IDN, ALU.add)
    ts("pk", whole("pk"), whole("m1"), -2.0 ** -10, None, ALU.mult)
    either("i20", "S", whole("i20"), IDN, 2.0 ** -20)
    either("n143", "S", whole("n143"), IDN, -143.0)
    either("nbig", "S", whole("nbig"), IDN, -2.0 ** 17)
    tt("tri", whole("tri"), TRIS, IDN, ALU.add)
    either("ntrif", "S", whole("ntrif"), whole("tri"), -1.0)
    either("blkn", "S", whole("blkn"), BLK, -1.0 / 256)
    either("b8f", "S", whole("b8f"), B8)
    ts("h0", whole("h0"), A("idn", 15, 128, 16), 14.0, None, ALU.mult)
    tt("h1", whole("h1"), whole("h0"), B8, ALU.add)
    fill("hb0", whole("hb"), 0.0)
    ts("hb", A("hb", 24, 32), whole("h1"), -0.5, None, ALU.mult)
    fill("rk0", A("rk", 0, 16, 1, 32), 0.0)
    tt("rk1", A("rk", 16, 144, 1, 32), A("rl", 16, 144, 1, 32), A("rl", 0, 128, 1, 32), ALU.add)
    ts("id1", whole("id1"), whole("id0"), 15, None, ALU.bitwise_and)
    ts("idv", whole("idv"), whole("id1"), 0.0, 16.0, ALU.is_equal, ALU.mult)
    ts("ids", whole("ids"), whole("id1"), 0.0, 128.0, ALU.is_equal, ALU.mult)
    cp("n16_0", A("n16", 0, C), whole("n0s"))

    for t in range(TK):
        T_, chs = "%d" % t, cut(cfg["chunks"][t])
        no, po, mo = t * C, t * R, 2 * t * C
        cp("sph" + T_, A("sph", no, no + C), A("sps", no, no + C))
        tt("spl" + T_, A("spl", no, no + C), A("sps", no, no + C), A("sph", no, no + C), ALU.subtract)
        send("n" + T_, A("nin", no, no + C), [A("n16", no, no + C)], 1)
        if t == 1:
            send("nh", A("nin", 3 * C, 4 * C), [A("n16", no, no + C)], 2)
        for k, (bias, scale) in enumerate([(0.0, 2.0 ** -7), (0.0, 2.0 ** -15), (0.0, 2.0)]):
            z, _m = turned("cd%d" % k + T_, chs, 8, [("uas", 0, 72, A("selt", 24 * t + 8 * k, 24 * t + 8 * k + 8, 1, 72))])
            act("cde"[k] + T_, A("cd", 3 * k * C + no, 3 * k * C + no + C), z, ACT.Identity, bias, scale)
        for ch in chs:
            J = "1_%d_%d" % (t, ch[2])
            either("gq" + J, "VS"[ch[2] & 1], wide("q1", ch, po), X(QR, small("n16", ch, no)), -1.0)
            either("gp" + J, "S", wide("pp", ch, po), X(whole("ptab"), small("n16", ch, no)))
            L, acc = draft(J, "q1", "pp", "i20", po, 2 * t, ch, "st1", "sc1"), pair("msg", ch, mo, 0)
            test(J, L, "1", small("cd", ch, no), acc, pair("msg", ch, mo, 1), ch)
            offsets("off" + J, "off1", to_rows("row" + J, ch, [], [(acc, IDN)]), "ra", ch, t)
        for ch in cut(cfg["dsend"]):
            send("d%d_%d" % (t, ch[2]), wide("din", ch, po), [wide("pp", ch, po), wide("q1", ch, po)], 1, 1)
        if t < TK - 1:
            send("p" + T_, A("pin", po, po + R), [A("pp", po, po + R)], 1)
        send("m" + T_, A("mi", mo, mo + 2 * C), [A("msg", mo, mo + 2 * C)], 1)
        for ch in chs:
            cp("X1_%d_%d" % (t, ch[2]), X(QW, small("off1", ch)), wide("pp", ch, po))
        for ch in thirds:
            either("r_%d_%d" % (t, ch[2]), "S", wide("rin", ch), wide("din", ch, po), 1.0, True)
            either("ge%d_%d" % (t, ch[2]), "S", wide("ecol", ch), X(whole("etab"), small("nin", ch, no)))
            if t == 1:
                prev = [add("h1_%d" % ch[2], "S", "act", (wide("hh", ch), X(whole("vtab"), small("nin", ch, 3 * C)),
                                                          ACT.Tanh, 0.0, 1.0), [wide("hh", ch)],
                            [X(whole("vtab"), small("nin", ch, 3 * C))], prev if ch[2] else ())]
            if t == 2:
                either("v2_%d" % ch[2], "S", wide("v2", ch), X(whole("vtab"), small("nin", ch, no)))
        if t == 2:
            dma("hadd", "G", whole("hh"), whole("v2"), "hadd", 128 * R * 4, True)
            for ch in thirds:
                act("h2_%d" % ch[2], wide("hh", ch), wide("hh", ch), ACT.Tanh)
        act("ab" + T_, whole("ab"), A("mi", mo, mo + 2 * C, 2), ACT.Copy, 0.0, 256.0)
        z, _m = turned("S" + T_, chs, 8, [("rin", 0, 128, B8)])
        tt("ds" + T_, whole("ds"), z, A("cd", 3 * C + no, 4 * C + no), ALU.mult)
        tt("xx" + T_, whole("xx"), whole("ds"), whole("ab"), ALU.max)
        for ch in chs:
            J, n = "2_%d_%d" % (t, ch[2]), ch[1] - ch[0]
            q, r, w = wide("q2", ch), wide("rin", ch), wide("ww", ch)
            g2 = either("gq" + J, "SV"[ch[2] & 1], q, X(QR, small("nin", ch, no)), -1.0)
            L = draft(J, "q2", "rin", "i20", 0, 2 * t + 1, ch, "st2", "sc2")
            z = A(temp(), 0, n)
            mm("sb" + J, [(z, [(whole("blkn"), r)])], soft=[g2])
            tt("sq" + J, z, z, q, ALU.mult)
            tt("z" + J, z, z, r, ALU.subtract)
            act("w" + J, w, z, ACT.Relu, 0.0, -1.0)
            acc, b2, p2 = pair("mi", ch, mo, 0), pair("bp", ch, 0, 0), pair("bp", ch, 0, 1)
            test(J, L, "2", small("xx", ch), b2, p2, ch)
            if t < TK - 1:
                offsets("off" + J, "off2", to_rows("row" + J, ch, [], [(acc, IDN), (b2, IDN)]), "rb", ch, t)
            z, _m = turned("c15" + J, [ch], 8, [("ww", 0, 128, whole("b8f"))])
            nb, th, hi = n // 128, small("th", ch), pair("hl", ch, 0, 0)
            rows = A("rt", 128 * ch[2], 128 * ch[2] + 128, 1, 16 * nb)
            tt("ec" + J, small("ec", ch), z, small("cd", ch, 6 * C + no), ALU.mult)
            ts("th" + J, th, small("ec", ch), 127.0 / 256, None, ALU.subtract)
            either("hi" + J, "V", hi, small("ec", ch))
            tt("lo" + J, pair("hl", ch, 0, 1), th, hi, ALU.subtract)
            z = summed("tr" + J, A(temp(), 0, 128, 1, 16 * nb),
                       [(pair("mi", ch, mo), whole("nbig")), (pair("bp", ch), whole("nbig"))], [(pair("hl", ch), IDN)])
            act("rt" + J, rows, z, ACT.Copy, 0.0, 1.0 / 256)
            z = A(temp(), 0, n)
            mm("cu" + J, [(z, [(whole("ntrif"), w)])], True, False)
            add("cv" + J, "P", "mm", [(A(z[1], b, n, nb), A("selb", 128 * b, 128 * b + 128, 1, 16 * nb), rows, False,
                                       b == nb - 1) for b in range(nb)], [z], [whole("selb"), rows])
            act("s3" + J, wide("s3", ch), z, ACT.Sign, 1.0 / 512)
            J = "3_%d_%d" % (t, ch[2])
            terms = [(pair("mi", ch, mo, 1), IDN), (acc, whole("n143")), (p2, IDN), (b2, whole("n143"))]
            third = [(A("hb", 24 - 8 * b, 24 - 8 * b + 8 * nb), x) for b, x in enumerate(blocks("s3", ch))]
            act("v" + J, rows_of("rv", ch), to_rows("row" + J, ch, terms, third), ACT.Identity, 15.0, -1.0)
            kj, e = small("k16", ch), wide("ecol", ch)
            cp("k16" + J, kj, to_list("k" + J, ch, [], from_rows("rk", "rv", ch)))
            if cfg["sele"][t][ch[2]] == "V":
                tt("sele" + J, wide("sele", ch), X(whole("idv"), kj), e, ALU.mult)
            else:
                act("hot" + J, wide("hot", ch), X(whole("ids"), kj), ACT.Copy)
                z = A(temp(), 0, n)
                mm("de" + J, [(z, [(IDN, e), (IDN, wide("hot", ch))])])
                act("sele" + J, wide("sele", ch), z, ACT.Relu, -2048.0, 16.0)
            z = to_list("nn" + J, ch, from_rows("rl", "rv", ch),
                        [(A("zz", 15 - m, 143 - m), A("sele", ch[0] + m, ch[1], 16)) for m in range(16)])
            cp("n" + J, small("n16", ch, no + C), z)
            act("nf" + J, small("nf", ch, no), z, ACT.Copy)
        if t < TK - 1:
            for ch in chs:
                cp("X2_%d_%d" % (t, ch[2]), X(QW, small("off2", ch)), wide("pin", ch, po))
    dma("st_n", "Y", D("yn"), whole("nf"), "st", 128 * C * 12)
    for ch in cut(cfg.get("tail", cfg["chunks"][2])):
        tt("v3_%d" % ch[2], wide("hs", ch), X(whole("vtab"), small("n16", ch, 3 * C)), wide("hh", ch), ALU.add)
        act("h3_%d" % ch[2], wide("ho", ch), wide("hs", ch), ACT.Tanh)
        dma("st_h%d" % ch[2], "Y", D("yh", ch[0], ch[1]), wide("ho", ch), "st", 128 * (ch[1] - ch[0]) * 4)
    return ops


COST = {"cycle": 0.83, "pe": 0.42, "gather": 1.5, "scatter": 3.2, "hop": 160.0, "dma": 1800.0, "hbm": 250.0,
        "send": 2000.0, "link": 70.0, "issue": 400.0, "first": 1500.0}
SPREAD = [{}, {"cycle": 1.2, "pe": 0.6, "gather": 1.9, "scatter": 5.0},
          {"gather": 1.2, "scatter": 2.2, "hop": 260.0, "link": 50.0, "send": 3000.0, "issue": 800.0}]
HEAT, REACH, PULL, STRIDE = 0.0006, 40, 0.5, 48


def cost_of(o, k):
    c, a = o["call"], o["args"]

    def narrow(x):
        return x[1][0] != "@" and SIZE[SB[x[1]][0]] == 2

    if c == "mm":
        return k["pe"] * sum(max(min(64, count_of(x)), count_of(y)) * (1 if narrow(x) else 4) for _o, x, y, _s, _e in a)
    if c in ("dma", "send"):
        return (k["issue"] if o["eng"] == "G" else 60.0) + (k["first"] if o["name"] in ("n0", "hadd") else 0.0)
    n = count_of(a[0])
    if o["name"] == "h1_0":
        n += 1300.0 / k["cycle"] / k["gather"]
    if c in ("sel", "iota"):
        return 170.0 + 2 * n * k["cycle"]
    aps = [x for x in a if isinstance(x, tuple)]
    if a[0][0] == "ind":
        return 50.0 + k["scatter"] * n * k["cycle"]
    if any(x[0] == "ind" for x in aps):
        return 60.0 + k["gather"] * n * k["cycle"]
    if c == "tt":
        n *= 1 if a[1][1][0] == "@" or a[2][1][0] == "@" else 2
    elif o["eng"] == "V" and all(narrow(x) for x in aps):
        n *= 0.5
    return max(64, n) * k["cycle"]


def schedule(ops, k, slack):
    n = len(ops)
    cost = [cost_of(o, k) for o in ops]
    lag = [k["hop"] if o["kind"] == "c" else
           (k["dma"] + o["nbytes"] / k["hbm"] if o["kind"] == "dma" else k["send"] + o["nbytes"] / k["link"]) for o in ops]
    after = [[] for _o in ops]
    for o in ops:
        for d in o["deps"] | o["soft"]:
            after[d].append(o["i"])
    way = [0.0] * n
    for i in reversed(range(n)):
        way[i] = cost[i] + lag[i] + max([way[j] for j in after[i]], default=0.0)
    users = {}
    for o in ops:
        for tp in o["temps"]:
            users.setdefault(tp, []).append(o["i"])
    left = [len(o["deps"] | o["soft"]) for o in ops]
    ready = [i for i in range(n) if not left[i]]
    done, began, free = {}, {}, {}
    bank_of, holder, order = {}, {}, []
    while ready:
        open_banks = sorted((max([done[u] for u in users.get(holder.get(b), [])], default=0.0), b) for b in range(8)
                            if all(u in done for u in users.get(holder.get(b), [])))
        cand = []
        for i in ready:
            o = ops[i]
            s = max([free.get(o["eng"], 0.0)] + [done[d] for d in o["deps"]] + [began[d] for d in o["soft"]])
            if any(tp not in bank_of for tp in o["temps"]):
                if not open_banks:
                    continue
                s = max(s, open_banks[0][0])
            cand.append((s, i))
        first = min(cand)
        s, i = max((c for c in cand if c[0] <= first[0] + slack and ops[c[1]]["eng"] == ops[first[1]]["eng"]),
                   key=lambda c: way[c[1]])
        o = ops[i]
        for tp in o["temps"]:
            if tp not in bank_of:
                b = open_banks[0][1]
                bank_of[tp], holder[b] = b, tp
        began[i], free[o["eng"]] = s, s + cost[i]
        done[i] = s + cost[i] + lag[i]
        order.append(i)
        ready.remove(i)
        for j in after[i]:
            left[j] -= 1
            if not left[j]:
                ready.append(j)
    return order


def refine(ops, order, steps, seed):
    n = len(ops)
    engines = "VSPGY"
    above = [0] * n
    need = []
    for o in ops:
        keep, seen = [], 0
        for d in sorted(o["deps"] | o["soft"], reverse=True):
            if not seen >> d & 1:
                keep.append(d)
            seen |= above[d] | 1 << d
        above[o["i"]] = seen
        need.append(keep)
    after = [[] for _o in ops]
    for i in range(n):
        for d in need[i]:
            after[d].append(i)
    users = {}
    for o in ops:
        for tp in o["temps"]:
            users.setdefault(tp, []).append(o["i"])
    opens = [[tp for tp in o["temps"] if users[tp][0] == o["i"]] for o in ops]
    eng = [engines.index(o["eng"]) for o in ops]
    either = [o["i"] for o in ops if o["call"] == "either"]
    sets = [dict(COST, **d) for d in SPREAD]
    cost = [[[cost_of(dict(o, eng=e), k) for e in "VS"] if o["call"] == "either" else [cost_of(o, k)] * 5 for o in ops]
            for k in sets]
    kind = [["c", "dma", "send"].index(o["kind"]) for o in ops]
    weak = [[d for d in need[i] if d in ops[i]["deps"] and d not in ops[i]["reads"] and not kind[i] and not kind[d]]
            for i in range(n)]
    firm = [[d for d in need[i] if d in ops[i]["deps"] and d not in weak[i]] for i in range(n)]

    def run(order, m, extra, marks, since):
        k, cm = sets[m], cost[m]
        hop, fixed, rate = k["hop"], [0.0, k["dma"], k["send"]], [1.0, k["hbm"], k["link"]]
        free, pipe, done, holder = [list(x) for x in marks[since]]
        first = m == 0
        del marks[since + 1:]
        for at in range(since * STRIDE, n):
            if at % STRIDE == 0 and at > since * STRIDE:
                marks.append((list(free), list(pipe), list(done), list(holder)))
            i = order[at]
            e = eng[i]
            s = free[e]
            for d in firm[i]:
                if done[d] > s:
                    s = done[d]
            for d in weak[i]:
                if eng[d] != e and done[d] > s:
                    s = done[d]
            if opens[i]:
                if first:
                    best = None
                    for b in range(8):
                        since_b = 0.0
                        for u in holder[b]:
                            if done[u] is None:
                                since_b = None
                                break
                            if done[u] > since_b:
                                since_b = done[u]
                        if since_b is not None and (best is None or since_b < best[0]):
                            best = (since_b, b)
                    if best is None:
                        return None
                    extra[i] = (best[1], holder[best[1]])
                    holder[best[1]] = users[opens[i][0]]
                for u in extra[i][1]:
                    if done[u] > s:
                        s = done[u]
            s += cm[i][e]
            free[e] = s
            if kind[i]:
                s = max(s + fixed[kind[i]], pipe[kind[i]]) + ops[i]["nbytes"] / rate[kind[i]]
                pipe[kind[i]] = s
                done[i] = s
            else:
                done[i] = s + hop
        return max(done) + PULL * sum(done) / n

    def value(order, extra, marks, since):
        extra, marks, total = dict(extra), [list(x) for x in marks], 0.0
        for m in range(len(sets)):
            t = run(order, m, extra, marks[m], since)
            if t is None:
                return None, extra, marks
            total += t / base[m]
        return total, extra, marks

    extra, marks = {}, [[([0.0] * 5, [0.0] * 3, [None] * n, [()] * 8)] for _k in sets]
    base = [run(order, m, extra, marks[m], 0) for m in range(len(sets))]
    now = float(len(sets))
    best = (now, list(order), list(eng), extra)
    rng = np.random.default_rng(seed)
    for step, (a, b, c, u) in enumerate(rng.random((steps, 4)).tolist()):
        if a < 0.04:
            i = either[int(b * len(either))]
            eng[i] = 1 - eng[i]
            new, low = order, order.index(i)
        else:
            at = int(b * n)
            i = order[at]
            lo = max([order.index(d) for d in need[i]], default=-1) + 1
            hi = min([order.index(d) for d in after[i]], default=n) - 1
            near = [p for p in range(max(lo, at - REACH), min(hi, at + REACH) + 1) if p != at and eng[order[p]] == eng[i]]
            if not near:
                continue
            new = order[:at] + order[at + 1:]
            new.insert(near[int(c * len(near))], i)
            low = min(at, near[int(c * len(near))])
        v, ex, mk = value(new, extra, marks, low // STRIDE)
        if v is not None and v <= now - HEAT * (1.0 - step / steps) * math.log(1.0 - u):
            now, order, extra, marks = v, new, ex, mk
            if v < best[0]:
                best = (v, list(order), list(eng), ex)
        elif a < 0.04:
            eng[i] = 1 - eng[i]
    bank_of = {}
    for o in ops:
        o["eng"] = engines[best[2][o["i"]]]
    for i, (b, before) in best[3].items():
        bank_of[opens[i][0]] = b
        ops[i]["deps"] = ops[i]["deps"] | set(before)
    return best[1], bank_of


def plan(cfg):
    ops = graph(cfg)
    order, bank_of = refine(ops, schedule(ops, COST, cfg["slack"]), cfg["steps"], cfg["seed"])
    pos, know, clock, need, cnt = {}, {}, {}, set(), {}
    for i in order:
        o = ops[i]
        e = o["eng"]
        k = know.setdefault(e, {})
        o["waits"] = []
        for d in sorted(o["deps"], key=lambda x: -pos[x][2]):
            line, at = pos[d][0], pos[d][1]
            if k.get(line, -1) >= at or (d not in o["reads"] and line == e and o["kind"] == "c"):
                continue
            o["waits"].append(d)
            need.add(d)
            for l2, a2 in clock[d].items():
                k[l2] = max(k.get(l2, -1), a2)
        line = e if o["kind"] == "c" else o["sem"]
        cnt[line] = cnt.get(line, -1) + 1
        pos[i] = (line, cnt[line], len(pos))
        clock[i] = {} if o["kind"] == "send" else dict(k)
        clock[i][line] = cnt[line]
    total = {}
    for i in order:
        o = ops[i]
        o["inc"] = o["kind"] != "c" or i in need
        if o["kind"] == "c" and o["inc"]:
            total[o["eng"]] = total.get(o["eng"], 0) + 1
            o["val"] = total[o["eng"]]
    return {"ops": ops, "order": order, "bank": bank_of, "total": total}


PLAN = plan(CFG)
SEMAPHORES = ["eV", "eS", "eP", "eG", "sent"] + sorted({o["sem"] for o in PLAN["ops"] if o["kind"] != "c"})


def rank_program(g, core, T, topo):
    rank = T.rank_of(core)
    if rank is None:
        return
    ops, N = PLAN["ops"], len(T.cores)
    queue = {"G": g, "V": g.vector, "S": g.scalar, "P": g.tensor, "Y": g.sync}

    def ap(x):
        if not isinstance(x, tuple):
            return x
        if x[0] == "ind":
            return ap(x[1]).indirect(ap(x[2]))
        if x[0] == "dram":
            return T[x[1]][:] if x[2] is None else T[x[1]][:, x[2]:x[3]]
        name = "bank%d" % PLAN["bank"][x[1]] if x[1][0] == "@" else x[1]
        if x[4] == 1:
            return T[name][0:x[5], x[2]:x[3]]
        return T[name][0:x[5], x[2]:x[3]:x[4]]

    def arrivals(hop):
        return len(topo.engines(T.cores[(rank - hop) % N], core))

    sent, stores = [0], [0]
    for i in PLAN["order"]:
        o = ops[i]
        q, c, a = queue[o["eng"]], o["call"], o["args"]
        for d in o["waits"]:
            od = ops[d]
            if od["kind"] == "c":
                q.wait_ge(T.sem["e" + od["eng"]], od["val"])
            else:
                q.wait_ge(T.sem[od["sem"]], 16 if od["kind"] == "dma" else arrivals(od["args"][2]))
        if c == "send":
            dst = T.cores[(rank + a[2]) % N]
            rid, pid, _se = topo.addr(dst)
            if a[3]:
                g.remote_dma_fused([RemoteDMATransfer(
                    dst_ids=[DstId(rid=rid, pnc=pid)], dma_engine_mask=topo.mask(core, dst), remote_sem=T.sem[o["sem"]],
                    srcs=[ap(x) for x in a[1]], dsts=[ap(a[0])], alu_op=a[3])], local_sem=T.sem["sent"])
            else:
                g.remote_dma(ap(a[0]), ap(a[1][0]), T.sem[o["sem"]], T.sem["sent"], pid, rid, topo.mask(core, dst))
            sent[0] += len(topo.engines(core, dst))
            continue
        if c == "dma":
            ins = q.dma_start(ap(a[0]), ap(a[1]), accum_op=ALU.add) if a[2] else q.dma_start(ap(a[0]), ap(a[1]))
            ins.then_inc(T.sem[o["sem"]], 16)
            stores[0] += 16 if o["sem"] == "st" else 0
            continue
        if c == "mm":
            for out, x, y, start, stop in a:
                ins = q.matmul(ap(out), ap(x), ap(y), start, stop)
        elif c == "tt":
            ins = q.tensor_tensor(ap(a[0]), ap(a[1]), ap(a[2]), a[3])
        elif c == "ts":
            if a[5] is None:
                ins = q.tensor_scalar(ap(a[0]), ap(a[1]), ap(a[2]), None, a[4])
            else:
                ins = q.tensor_scalar(ap(a[0]), ap(a[1]), ap(a[2]), ap(a[3]), a[4], a[5])
        elif c == "cp":
            ins = q.tensor_copy(ap(a[0]), ap(a[1]))
        elif c == "scan":
            ins = q.tensor_tensor_scan(ap(a[0]), ap(a[1]), ap(a[2]), 0.0, ALU.mult, ALU.max)
        elif c == "act":
            ins = q.activation(ap(a[0]), ap(a[1]), a[2], bias=a[3], scale=a[4])
        elif c == "either" and o["eng"] == "S":
            ins = q.activation(ap(a[0]), ap(a[1]), ACT.Relu if a[3] else ACT.Copy, bias=0.0, scale=a[2])
        elif c == "either":
            ins = q.tensor_scalar(ap(a[0]), ap(a[1]), 0.0 if a[3] else a[2], None, ALU.max if a[3] else ALU.mult)
        elif c == "fill":
            ins = q.memset(ap(a[0]), a[1])
        elif c == "sel":
            ins = q.affine_select(ap(a[0]), ap(a[1]), a[2], a[3], 0.0, a[4], a[5])
        elif SB[a[0][1]][0] == I32:
            ins = q.iota(ap(a[0]), a[1], a[2], a[3])
        else:
            ins = q.iota(ap(a[0]), a[1], a[2], a[3], allow_small_or_imprecise_dtypes=True)
        if o["inc"]:
            ins.then_inc(T.sem["e" + o["eng"]], 1)
    for e, v in PLAN["total"].items():
        g.wait_ge(T.sem["e" + e], v)
    g.wait_ge(T.sem["sent"], sent[0])
    g.sync.wait_ge(T.sem["st"], stores[0])
